import numpy as np, ml_dtypes
CORES = [9,25,41,57]
N = 4
import mx_ref
BF = ml_dtypes.bfloat16
def gentries(a):
    return np.ascontiguousarray(a.reshape(8, 16, -1).transpose(0, 2, 1)).reshape(8, -1)
def gtable(e):
    e = np.asarray(e); return np.ascontiguousarray(e.reshape(8, -1, 16).transpose(0, 2, 1)).reshape(128, -1).astype(np.int32)
def gcols(t, e):
    v = np.concatenate([t.reshape(8, 16, -1, 4), np.zeros((8, 16, 1, 4), BF)], axis=2)
    return np.ascontiguousarray(np.stack([v[g][:, e[g]] for g in range(8)])).reshape(128, -1)
def tile(rs):
    return np.stack(rs, axis=2).reshape(128, -1).astype(BF)
def pick(q, e):
    c = np.concatenate([q[0].reshape(128, -1, 4), np.zeros((128, 1, 4), np.uint8)], axis=1); s = np.concatenate([q[1], np.ones((16, 1), np.uint8)], axis=1)
    return (np.ascontiguousarray(c[:, e].reshape(128, -1)), np.ascontiguousarray(s[:, e]))
def join(*qs):
    return (np.concatenate([q[0] for q in qs], axis=1), np.concatenate([q[1] for q in qs], axis=1))
def put(q, e, v):
    c, s = q[0].reshape(128, -1, 4).copy(), q[1].copy(); c[:, e] = v[0].reshape(128, -1, 4); s[:, e] = v[1]
    return (c.reshape(128, -1), s)
def pk(c, s):
    return (np.ascontiguousarray(c), mx_ref.live(s))
def emit(q):
    return q[0], q[1]
def packed(v, rng):
    q = [mx_ref.quantize(np.ascontiguousarray(v[r])) for r in range(N)]
    return np.stack([a for a, b in q]), np.stack([mx_ref.plane(b, rng) for a, b in q])
def values_of_codes():
    e, c = np.zeros((128, 128, 4), np.float32), np.zeros((128, 2, 4), np.uint8)
    e[np.arange(128), np.arange(128), 0] = 1
    c[:127, :, 0] = np.arange(256).reshape(2, 128).T[:127]
    return mx_ref.matmul(mx_ref.quantize(e.reshape(128, 512).astype(BF)), (c.reshape(128, 8), np.full((16, 2), 127, np.uint8))).T.reshape(-1).astype(np.float64)
CODE_VALUE, SCALE_VALUE = values_of_codes(), 2.0 ** (np.arange(256) - 127.0)
def decode(q):
    return (CODE_VALUE[q[0]].reshape(16, 8, -1, 4) * SCALE_VALUE[q[1]][:, None, :, None] + 0.0).reshape(128, -1).astype(np.float32)
def f(rng, *shape):
    return mx_ref.flush((rng.standard_normal(shape, dtype=np.float32) * np.exp2(rng.integers(-2, 3, shape[:-1] + (1,)))).astype(BF))
def wide(rng, *shape, cols=0):
    v = rng.standard_normal(shape, dtype=np.float32) * np.exp2(rng.integers(-12, 13, shape)).astype(np.float32)
    if cols: v *= np.repeat(np.exp2(rng.integers(-cols, cols + 1, shape[:-2] + (1, shape[-1] // 4))) * (rng.random(shape[:-2] + (1, shape[-1] // 4)) > 0.0625), 4, axis=-1).astype(np.float32)
    return mx_ref.flush(v.astype(BF))
C, K, R = 320, 80, 3
def rings(o):
    e = np.zeros((N, 8, C), int)
    np.put_along_axis(e, o, np.roll(o, -1, axis=2), axis=2)
    return np.stack([gtable(e[r]) for r in range(N)])
def orders(rng):
    return np.argsort(rng.random((N, 8, C)), axis=2)
def numbers_of(rng):
    return {"x": np.array(f(rng, N, 128, 4 * C)), "u": np.array(f(rng, N, 128, 512)), "v": np.array(f(rng, N, 128, 512))}
def layers(rng):
    return np.array(f(rng, N, 128, 2048)).reshape(N, 8, 16, 4, 8, 16, 4)
def carry(source, size):
    w = np.zeros((N, 128, 4, 128, 4), np.float32)
    i = np.arange(128)
    for b in range(4): w[:, i - i % 16 + np.array(source)[i % 16], b, i, b] = 32 * np.resize(size, 128)
    return w.astype(BF)
def weights(rng, w):
    c, p = packed(np.ascontiguousarray(w).reshape(N, 128, 2048), rng)
    return {"wc": c, "ws": p}
def signs(rng):
    return np.stack([rng.permutation(8) % 2 * 2.0 - 1.0 for r in range(N)])
def setup_inputs(rng):
    return {**numbers_of(rng), **weights(rng, layers(rng)), "nx": rings(orders(rng))}
def setup_inputs_ties(rng):
    d = numbers_of(rng)
    x = d["x"].astype(np.float32).reshape(N, 8, 16, C, 4)
    e = (rng.integers(N) + np.arange(N)) % N
    w = layers(rng)
    o = orders(rng)
    for i in range(N):
        r = e[i]
        k = np.stack([rng.permutation(C) % 3 - 1 for g in range(8)])
        if i < 2: k[:] = i
        x[r][:, :8] = np.abs(x[r][:, :8, :1]) * k[:, None, :, None]
        if i >= 3 and i % 2 == 1: w[r][:, :, :, :, :8] = 0
        g = rng.permutation(8)
        o[r, g[0]] = np.arange(C)
        o[r, g[1]] = np.arange(C)[::-1]
    u = d["u"].astype(np.float32).reshape(N, 8, 16, 8, 16, 4)
    k = np.abs(u)
    u[:, :, :, :, 0] = 0
    for g in range(8): u[:, g, :8, g, 0] = k[:, g, :8, g, 0]
    return {"x": x.reshape(N, 128, 4 * C).astype(BF), "u": u.reshape(N, 128, 512).astype(BF), "v": d["v"], **weights(rng, w), "nx": rings(o)}
def setup_inputs_near(rng):
    d = numbers_of(rng)
    x = d["x"].astype(np.float32).reshape(N, 8, 16, C, 4)
    x[:, :, :2] = 0
    u = d["u"].reshape(N, 128, 128, 4)
    u[:, :, ::16] = 0
    e = rng.permutation(8)
    for g in range(8):
        if e[g] < 4:
            s, size, k = rng.integers(-2, 3, (N, 2, C)), 2.0 ** -30, 2.0 ** -30
        else:
            s, size, k = rng.integers(0, 16, (N, 2, C)), 2.0 ** -23, 1.0
            x[:, g, 0, :, 0] = rng.choice([-1.0, 1.0], (N, C))
            x[:, g, 1, :, 0] = e[g] % 2 * 2.0 - 1.0
        x[:, g, 8:10] = ((np.abs(s)[..., None] >> np.arange(4)) & 1) * np.sign(s)[..., None] * np.exp2(np.arange(4.0)) * size
        x[:, g, 10:] = rng.integers(4, 8, (N, 6, C, 4)) * 2 * size
        u[:, 16 * g, 16 * g, 0] = k
        u[:, 16 * g + 8, 16 * g] = k
    times = np.resize(np.array([1.0, 1.0] + [0.75] * 6 + [1.0, 1.0] + [0.75] * 6), (8, 16))
    times[e < 4, 8:10] = 2.0 ** -7
    w = carry([1, 1, 2, 3, 4, 5, 6, 7, 9, 8, 10, 11, 12, 13, 14, 15], times)
    return {"x": x.reshape(N, 128, 4 * C).astype(BF), "u": u.reshape(N, 128, 512), "v": d["v"], **weights(rng, w), "nx": rings(orders(rng))}
def setup_inputs_huge(rng):
    d = numbers_of(rng)
    x = 2.0 ** 30 * (0.8 + 0.2 * rng.random((N, 8, 16, C, 4)))
    for r in range(N): x[r, :, :8] *= (rng.permutation(C) % 2 * 2.0 - 1.0)[:, None]
    u = d["u"].reshape(N, 8, 16, 8, 16, 4)
    u[:, :, :, :, 0] = 0
    a = 2.0 ** 30 * (0.8 + 0.2 * rng.random((N, 8, 8, 8, 4))) * signs(rng)[:, None, None, :, None]
    u[:, :, :8, :, 0] = a.astype(np.float32).astype(BF)
    w = carry([8, 9, 10, 11, 12, 13, 14, 15, 0, 1, 2, 3, 4, 5, 6, 7], [0.875] * 16)
    o = np.zeros((N, 8, C), int) + rng.permutation(C)
    return {"x": x.astype(np.float32).reshape(N, 128, 4 * C).astype(BF), "u": u.reshape(N, 128, 512), "v": d["v"], **weights(rng, w), "nx": rings(o)}
def setup_inputs_slots(rng):
    d = numbers_of(rng)
    n = [0, 1, C // 2, K + 1, K, K - 1, K, K + 1]
    e = rng.permutation(8)
    o = orders(rng)
    x = d["x"].astype(np.float32).reshape(N, 8, 16, C, 4)
    for r in range(N):
        for g in range(8):
            turns = np.sort(rng.permutation(C)[:2 * n[(e[g] + r) % 8]])
            s = (np.searchsorted(turns, np.arange(C), side="right") + rng.integers(2)) % 2
            x[r, g, 0][o[r, g], 0] = 2.0 * s - 1.0
    u = d["u"].reshape(N, 128, 128, 4)
    u[:, :, ::16] = 0
    for h in range(0, 128, 16): u[:, h, h, 0] = 1
    return {"x": x.reshape(N, 128, 4 * C).astype(BF), "u": u.reshape(N, 128, 512), "v": d["v"], **weights(rng, layers(rng)), "nx": rings(o)}
def setup_inputs_spread(rng):
    d = setup_inputs(rng)
    d["x"] = wide(rng, N, 128, 4 * C, cols=6)
    return d
def check_inputs(d):
    b = []
    for k in ("x", "u", "v"):
        a = np.abs(d[k].astype(np.float32))
        if not (np.isfinite(a).all() and ((a == 0) | (a >= 2.0 ** -30) & (a <= 2.0 ** 30)).all()): b.append("a value of " + k)
    if ((d["wc"] & 0x7F) == 0x7F).any(): b.append("a code of wc that is no number")
    z = np.zeros((128, 4, 4), np.float32)
    z[:, 1] = 2.0 ** -30
    z[:, 2] = 2.0 ** 30
    c, s = emit(mx_ref.quantize(z.reshape(128, 16).astype(BF)))
    for r in range(N):
        p = mx_ref.live(d["ws"][r])
        if not ((p == s[0, 0]) | (p >= s[0, 1]) & (p <= s[0, 2])).all(): b.append("a scale of ws")
        e = gentries(d["nx"][r])
        good = bool(((e >= 0) & (e < C)).all())
        j = np.zeros(8, int)
        for i in range(C):
            if good:
                j = e[np.arange(8), j]
                good = bool(((j == 0) == (i == C - 1)).all())
        if not good: b.append("a ring of nx")
    return b
def reference(x, u, v, wc, ws, nx):
    qu = [mx_ref.quantize(u[r]) for r in range(N)]
    lay = [pk(wc[r], ws[r]) for r in range(N)]
    after = [gentries(nx[r]) for r in range(N)]
    before = [np.argsort(after[r], axis=1) for r in range(N)]
    now = [x[r] for r in range(N)]
    for t in range(R):
        forward, parts, sent, count = [], [], [], []
        for r in range(N):
            q = mx_ref.quantize(now[r])
            a = mx_ref.matmul(qu[r], q)[::16] > 0
            p = decode(q).astype(BF)
            e, n = np.full((8, 2 * K), -1), np.zeros(8, int)
            for g in range(8):
                j = np.flatnonzero(a[g] & ~a[g][after[r][g]])[:K]
                n[g] = len(j)
                e[g, 0:2 * len(j):2] = j
                e[g, 1:2 * len(j):2] = after[r][g][j]
            forward.append(a)
            parts.append(p)
            sent.append(mx_ref.quantize(gcols(p, e)))
            count.append(n)
        made, lists = [], []
        for r in range(N):
            z, n = sent[r - 1], count[r - 1]
            h = tile([mx_ref.matmul(pick(lay[r], np.arange(128 * b, 128 * b + 128)), z) * np.float32(0.03125) for b in range(4)])
            p = mx_ref.matmul(qu[r], mx_ref.quantize(h))[::16]
            swap = (p[:, 1::2] > p[:, 0::2]).astype(int)
            e = np.where(forward[r], before[r], after[r])
            for g in range(8):
                a, o = forward[r][g], after[r][g]
                j = np.flatnonzero(~a & a[o])
                e[g, j] = j
                e[g, o[j]] = o[j]
                j = j[:n[g]]
                k = np.arange(len(j))
                e[g, j] = C + 2 * k + swap[g, k]
                e[g, o[j]] = C + 2 * k + 1 - swap[g, k]
            made.append(gcols(np.concatenate([parts[r], h], axis=1), e))
            lists.append(e)
        now = made
    y, ot = np.zeros((N, 128, C), np.float32), np.zeros((N, 8, C), np.float32)
    oc, osc = np.zeros((N, 128, 4 * C), np.uint8), np.zeros((N, 16, C), np.uint8)
    for r in range(N):
        q = mx_ref.quantize(now[r])
        y[r] = mx_ref.matmul(mx_ref.quantize(v[r]), q)
        ot[r] = lists[r]
        oc[r], osc[r] = emit(q)
    return {"y": y, "ot": ot, "oc": oc, "osc": osc}

@@ -1,0 +1,460 @@
+import numpy as np
+from concourse.mybir import dt, AluOpType, AxisListType, ActivationFunctionType
+
+ALU = AluOpType
+ACT = ActivationFunctionType
+C, K, R, N = 320, 80, 3, 4
+CUT = (0, 192, C)
+P2 = 2 * K
+TW = C + P2
+AW = C + 16
+OFF, BIG = 1024.0, 4096.0
+HALF = "float16"
+
+
+def _layout(sizes, align):
+    at, pos = {}, 0
+    for name, n in sizes:
+        at[name] = pos
+        pos += -(-n // align) * align
+    return at, pos
+
+
+LB, LBW = _layout([("F", C), ("F2", C), ("M", C), ("C", C), ("B", C), ("CB", C), ("CBP", C), ("I", C), ("JS", 3 * C)], 16)
+LH, LHW = _layout([("NXA", K), ("NXR", K), ("RAW", 5 * C), ("V", C), ("VR", C)], 16)
+LF, LFW = _layout([("HB", C), ("ACC", 8), ("PS", K), ("W5", 100), ("PR", 40), ("KK", 40), ("X60", 60), ("Y", 20), ("Y2", 20),
+                   ("Z", 20), ("ZC", 20), ("DT", 40), ("U", 40), ("MM", 40), ("RR", 40), ("NP", 2)], 8)
+
+X4 = "float8_e4m3fn_x4"
+SCRATCH = {
+    "iotaf": ("sbuf", [128, TW], "float32"), "mi": ("sbuf", [128, 16], "int32"), "mj": ("sbuf", [128, 16], "int32"),
+    "m0": ("sbuf", [128, 16], HALF), "m1": ("sbuf", [128, 16], HALF), "dmask": ("sbuf", [128, C], HALF),
+    "pi": ("sbuf", [128, 20], "int32"), "pj": ("sbuf", [128, 20], "int32"), "j0": ("sbuf", [128, 20], "int32"),
+    "jw": ("sbuf", [128, 20], "float32"), "offp": ("sbuf", [128, 2], "float32"), "kb": ("sbuf", [128, 8], "float32"),
+    "uli": ("sbuf", [128, 8], "int32"), "ul": ("sbuf", [128, 8], "uint16"),
+    "ones": ("sbuf", [128, 128], "bfloat16"), "eb": ("sbuf", [128, 516], "bfloat16"),
+    "ec": ("sbuf", [128, 512], X4), "es": ("sbuf", [128, 512], "uint8"),
+    "ut": ("sbuf", [128, 512], "bfloat16"), "uc": ("sbuf", [128, 128], X4), "us": ("sbuf", [128, 128], "uint8"),
+    "upc": ("sbuf", [128, 128], X4), "ups": ("sbuf", [128, 128], "uint8"),
+    "vt": ("sbuf", [128, 512], "bfloat16"), "vc": ("sbuf", [128, 128], X4), "vs": ("sbuf", [128, 128], "uint8"),
+    "lwc": ("sbuf", [128, 512], X4), "lws": ("sbuf", [128, 512], "uint8"),
+    "nxi": ("sbuf", [128, 20], "int32"), "nx16": ("sbuf", [128, 20], "uint16"), "nxw": ("sbuf", [128, 20], "float32"),
+    "nxf": ("sbuf", [128, AW], "float32"), "pvf": ("sbuf", [128, C], "float32"), "pvr": ("sbuf", [128, C], "float32"),
+    "pvw": ("sbuf", [128, 20], "float32"), "pv16": ("sbuf", [128, 20], "uint16"), "cj": ("sbuf", [128, 60], "float32"),
+    "cz": ("sbuf", [128, 20], "float32"),
+    "ta": ("sbuf", [128, 4 * AW], "bfloat16"), "wd": ("sbuf", [128, 176], "bfloat16"),
+    "jv": ("sbuf", [128, 2 * AW], "bfloat16"), "o2": ("sbuf", [128, 40], "float32"),
+    "lb": ("sbuf", [128, R * LBW], "bfloat16"), "lf": ("sbuf", [128, R * LFW], "float32"), "lh": ("sbuf", [128, R * LHW], HALF),
+    "yt": ("sbuf", [128, C], "float32"), "ott": ("sbuf", [128, C], "float32"),
+}
+for _t in range(R + 1):
+    SCRATCH["x%d" % _t] = ("sbuf", [128, 4 * C], "bfloat16")
+    SCRATCH["qc%d" % _t] = ("sbuf", [128, C], X4)
+    SCRATCH["qs%d" % _t] = ("sbuf", [128, C], "uint8")
+for _t in range(R):
+    SCRATCH["tp%d" % _t] = ("sbuf", [128, 4 * TW], "bfloat16")
+    SCRATCH["lc%d" % _t] = ("sbuf", [128, C], X4)
+    SCRATCH["ls%d" % _t] = ("sbuf", [128, C], "uint8")
+    SCRATCH["at%d" % _t] = ("sbuf", [128, 4 * P2], "bfloat16")
+    SCRATCH["ac%d" % _t] = ("sbuf", [128, P2], X4)
+    SCRATCH["as%d" % _t] = ("sbuf", [128, P2], "uint8")
+    SCRATCH["ht%d" % _t] = ("sbuf", [128, 4 * P2], "bfloat16")
+    SCRATCH["hc%d" % _t] = ("sbuf", [128, P2], X4)
+    SCRATCH["hs%d" % _t] = ("sbuf", [128, P2], "uint8")
+    SCRATCH["sl%d" % _t] = ("sbuf", [128, 12], "uint16")
+    SCRATCH["ll%d" % _t] = ("sbuf", [128, 12], "uint16")
+    SCRATCH["hk%d" % _t] = ("sbuf", [128, 40], "uint16")
+    SCRATCH["h%d" % _t] = ("sbuf", [128, 20], "uint16")
+for _b in range(8):
+    SCRATCH["ps%d" % _b] = ("psum", [128, 512], "float32")
+
+SEMAPHORES = (["cv", "cs", "ct", "cg", "loc"] + ["d%d" % i for i in range(20)]
+              + [s + "%d" % t for t in range(R) for s in ("ra", "rb", "rs", "rl")])
+
+
+def _cols(a, b, step=1):
+    m = 0
+    for c in range(a, b, step):
+        m |= 1 << c
+    return m
+
+
+def _machine(g, T):
+    queues = {"v": g.vector, "s": g.scalar, "t": g.tensor, "g": g, "y": g.sync}
+    total, clock, hist, fresh = {}, {}, {}, [0]
+    known = dict((q, {}) for q in queues)
+
+    def wait(q, sem, val):
+        if known[q].get(sem, 0) >= val:
+            return
+        queues[q].wait_ge(T.sem[sem], val)
+        for s, n in clock.get((sem, val), {}).items():
+            known[q][s] = max(known[q].get(s, 0), n)
+        known[q][sem] = max(known[q].get(sem, 0), val)
+
+    def order(q, writes, reads):
+        need = {}
+        for acc, wr in [(a, True) for a in writes] + [(a, False) for a in reads]:
+            for mask, oq, sem, val, owr in hist.get(acc[1], []):
+                if not mask & acc[2]:
+                    continue
+                if wr and not owr and oq == q:
+                    continue
+                if not wr and not owr and (oq == q or not acc[1].startswith("ps")):
+                    continue
+                need[sem] = max(need.get(sem, 0), val)
+        need = [(s, n) for s, n in need.items() if known[q].get(s, 0) < n]
+        for s, n in need:
+            if not any(clock.get(o, {}).get(s, 0) >= n for o in need if o != (s, n)):
+                wait(q, s, n)
+
+    def note(q, sem, val, writes, reads):
+        for a in writes:
+            hist.setdefault(a[1], []).append((a[2], q, sem, val, True))
+        for a in reads:
+            hist.setdefault(a[1], []).append((a[2], q, sem, val, False))
+
+    def op(q, call, writes, reads):
+        order(q, writes, reads)
+        sem = "c" + q
+        val = total[sem] = total.get(sem, 0) + 1
+        call(queues[q]).then_inc(T.sem[sem], 1)
+        clock[(sem, val)] = dict(known[q])
+        note(q, sem, val, writes, reads)
+
+    def dma(q, out, in_, writes, reads):
+        order(q, writes, reads)
+        sem = "d%d" % fresh[0]
+        fresh[0] += 1
+        total[sem] = 16
+        queues[q].dma_start(out, in_).then_inc(T.sem[sem], 16)
+        clock[(sem, 16)] = dict(known[q])
+        note("d", sem, 16, writes, reads)
+
+    def send(out, in_, rsem, where, reads, engines):
+        order("g", [], reads)
+        total["loc"] = total.get("loc", 0) + engines
+        g.remote_dma(out, in_, T.sem[rsem], T.sem.loc, where[0], where[1], where[2])
+
+    def lands(writes, rsem, engines):
+        total[rsem] = engines
+        note("net", rsem, engines, writes, [])
+
+    def close():
+        for sem in sorted(total):
+            wait("g", sem, total[sem])
+
+    return op, dma, send, lands, close
+
+
+def rank_program(g, core, T, topo):
+    rank = T.rank_of(core)
+    if rank is None:
+        return
+    op, dma, send, lands, close = _machine(g, T)
+    dst, src = T.cores[(rank + 1) % N], T.cores[rank - 1]
+    rid, pid = topo.addr(dst)[:2]
+    where = (pid, rid, topo.mask(core, dst))
+    n_out, n_in = len(topo.engines(core, dst)), len(topo.engines(src, core))
+
+    def A(name, a, b, step=1):
+        return (T[name][:, a:b:step] if step > 1 else T[name][:, a:b], name, _cols(a, b, step))
+
+    def lb(t, key, n, a=0, step=1):
+        o = t * LBW + LB[key]
+        return A("lb", o + a, o + n, step)
+
+    def lf(t, key, n, a=0, step=1):
+        o = t * LFW + LF[key]
+        return A("lf", o + a, o + n, step)
+
+    def lh(t, key, n, a=0, step=1):
+        o = t * LHW + LH[key]
+        return A("lh", o + a, o + n, step)
+
+    def U8(acc):
+        return acc[0].bitcast(dt.uint8)
+
+    def E(b):
+        return A("ec", 128 * b, 128 * b + 128), A("es", 128 * b, 128 * b + 128)
+
+    def W(b):
+        return A("lwc", 128 * b, 128 * b + 128), A("lws", 128 * b, 128 * b + 128)
+
+    def fill(out, value):
+        op("v", lambda q: q.memset(out[0], value), [out], [])
+
+    def copy(out, in_):
+        op("v", lambda q: q.tensor_copy(out[0], in_[0]), [out], [in_])
+
+    def pick(q, out, win, off):
+        if q == "v":
+            op("v", lambda e: e.tensor_copy(out[0], win[0].indirect(off[0])), [out], [win, off])
+        else:
+            op("s", lambda e: e.activation(out[0], win[0].indirect(off[0]), ACT.Copy), [out], [win, off])
+
+    def scalar1(out, in0, s1, op0, s2=None, op1=None):
+        reads = [in0] + ([s1] if isinstance(s1, tuple) else [])
+        a1 = s1[0] if isinstance(s1, tuple) else s1
+        if op1 is None:
+            op("v", lambda q: q.tensor_scalar(out[0], in0[0], a1, None, op0), [out], reads)
+        else:
+            op("v", lambda q: q.tensor_scalar(out[0], in0[0], a1, s2, op0, op1), [out], reads)
+
+    def two(out, in0, in1, o):
+        op("v", lambda q: q.tensor_tensor(out[0], in0[0], in1[0], o), [out], [in0, in1])
+
+    def two_at(out, win, off, in1, o):
+        op("v", lambda q: q.tensor_tensor(out[0], win[0].indirect(off[0]), in1[0], o), [out], [win, off, in1])
+
+    def scan(out, d0, d1, op0, op1):
+        op("v", lambda q: q.tensor_tensor_scan(out[0], d0[0], d1[0], 0.0, op0, op1), [out], [d0, d1])
+
+    def diagonal(raw, rows, n):
+        scan(raw, A("dmask", 0, n), rows, ALU.add, ALU.max)
+
+    def quant(c, s, tile):
+        op("v", lambda q: q.quantize_mx(c[0], s[0], tile[0]), [c, s], [tile])
+
+    def mm(bank, w, xc, xs, n):
+        out = A("ps%d" % bank, 0, n)
+        op("t", lambda q: q.matmul_mx(out[0], w[0][0], w[1][0], xc[0], xs[0], True, True), [out], [w[0], w[1], xc, xs])
+
+    def act(out, in_, scale=None):
+        if scale is None:
+            op("s", lambda q: q.activation(out[0], in_[0], ACT.Copy), [out], [in_])
+        else:
+            op("s", lambda q: q.activation(out[0], in_[0], ACT.Copy, scale=scale), [out], [in_])
+
+    def load(q, name, a, b, ap):
+        w = A(name, a, b)
+        dma(q, w[0], ap, [w], [])
+
+    def iota(out, pattern, base, ch):
+        op("g", lambda q: q.iota(out[0], pattern, base, ch), [out], [])
+
+    def iota_f(out, step, n, base):
+        op("g", lambda q: q.iota(out[0], [[step, n]], base, 0, allow_small_or_imprecise_dtypes=True), [out], [])
+
+    def state_codes(t, h):
+        a, b = CUT[h], CUT[h + 1]
+        quant(A("qc%d" % t, a, b), A("qs%d" % t, a, b), A("x%d" % t, 4 * a, 4 * b))
+
+    def send_codes(t, h):
+        i = A("qc%d" % t, CUT[h], CUT[h + 1])
+        send(U8(A("lc%d" % t, CUT[h], CUT[h + 1])), U8(i), ("ra%d", "rb%d")[h] % t, where, [i], n_out)
+
+    def send_scales(t):
+        i = A("qs%d" % t, 0, C)
+        send(A("ls%d" % t, 0, C)[0], i[0], "rs%d" % t, where, [i], n_out)
+
+    load("y", "nxi", 0, 20, T.nx[:, :])
+    load("s", "ut", 0, 512, T.u[:, :])
+    load("y", "x0", 0, 4 * CUT[1], T.x[:, 0:4 * CUT[1]])
+    load("y", "x0", 4 * CUT[1], 4 * C, T.x[:, 4 * CUT[1]:4 * C])
+    w = A("lwc", 0, 512)
+    dma("y", U8(w), T.wc[:, :], [w], [])
+    load("s", "lws", 0, 512, T.ws[:, :])
+    load("y", "vt", 0, 512, T.v[:, :])
+    for t in range(R):
+        lands([A("lc%d" % t, 0, CUT[1])], "ra%d" % t, n_in)
+        lands([A("lc%d" % t, CUT[1], C)], "rb%d" % t, n_in)
+        lands([A("ls%d" % t, 0, C)], "rs%d" % t, n_in)
+        lands([A("ll%d" % t, 0, 12)], "rl%d" % t, n_in)
+
+    fill(A("ones", 0, 128), 1.0)
+    fill(A("eb", 0, 516), 0.0)
+    iota(A("uli", 0, 8), [[16, 8]], 0, 0)
+    iota(A("mi", 0, 16), [[1, 16]], 128, -1)
+    iota(A("pi", 0, 20), [[0, 20]], 0, 1)
+    iota(A("j0", 0, 20), [[16, 20]], 0, 0)
+    e, o = A("eb", 3, 515, 4), A("ones", 0, 128)
+    op("g", lambda q: q.affine_select(e[0], o[0], [[-1, 128]], ALU.is_equal, 0.0, 0, 1), [e], [o])
+    iota_f(A("iotaf", 0, TW), 1, TW, 0)
+    for b in range(2):
+        iota_f(A("jv", AW * b + C, AW * b + C + 8), 0, 8, -C)
+    copy(A("ul", 0, 8), A("uli", 0, 8))
+    scalar1(A("mj", 0, 16), A("mi", 0, 16), 15, ALU.bitwise_and)
+    scalar1(A("pj", 0, 20), A("pi", 0, 20), 15, ALU.bitwise_and)
+    scalar1(A("m0", 0, 16), A("mj", 0, 16), 0.0, ALU.is_equal, -BIG, ALU.mult)
+    scalar1(A("m1", 0, 16), A("mj", 0, 16), 1.0, ALU.is_equal, OFF, ALU.mult)
+    two(A("jw", 0, 20), A("j0", 0, 20), A("pj", 0, 20), ALU.add)
+    two(A("dmask", 0, 16), A("m0", 0, 16), A("m1", 0, 16), ALU.add)
+    scalar1(A("offp", 0, 2), A("pj", 0, 2), 14.5, ALU.is_lt, OFF, ALU.mult)
+    for b in range(4):
+        quant(E(b)[0], E(b)[1], A("eb", 3 - b, 515 - b))
+        copy(A("dmask", 16 << b, 32 << b), A("dmask", 0, 16 << b))
+    fill(A("nxf", C, AW), float(C))
+    copy(A("dmask", 256, C), A("dmask", 0, C - 256))
+    scalar1(A("kb", 0, 5), A("jw", 0, 5), 0.5, ALU.add)
+    copy(A("nx16", 0, 20), A("nxi", 0, 20))
+    copy(A("nxw", 0, 20), A("nxi", 0, 20))
+    scalar1(A("cz", 0, 20), A("jw", 0, 20), -1.0, ALU.mult, C - 2.0, ALU.add)
+    quant(A("uc", 0, 128), A("us", 0, 128), A("ut", 0, 512))
+    up, ic_, ul = (A("upc", 0, 128), A("ups", 0, 128)), A("uc", 0, 128), A("ul", 0, 8)
+    op("v", lambda q: q.tensor_copy(up[0][0].bitcast(dt.uint32), ic_[0].bitcast(dt.uint32).indirect(ul[0])), [up[0]], [ic_, ul])
+    pick("s", up[1], A("us", 0, 128), ul)
+    state_codes(0, 0)
+    send_codes(0, 0)
+    state_codes(0, 1)
+    pick("s", A("nxf", 0, C), A("iotaf", 0, C), A("nx16", 0, 20))
+    offp, nx16, pv16, nxw, jw, pvw = A("offp", 0, 1), A("nx16", 0, 20), A("pv16", 0, 20), A("nxw", 0, 20), A("jw", 0, 20), A("pvw", 0, 20)
+
+    for t in range(R):
+        n = lambda s: "%s%d" % (s, t)
+        qc, qs = A(n("qc"), 0, C), A(n("qs"), 0, C)
+        F, F2, M, Cn, B = lb(t, "F", C), lb(t, "F2", C), lb(t, "M", C), lb(t, "C", C), lb(t, "B", C)
+        CB, CBP, I, W5, KK, O2 = lb(t, "CB", C), lb(t, "CBP", C), lb(t, "I", C), lf(t, "W5", 100), lf(t, "KK", 20), A("o2", 0, 20)
+
+        def raw(i):
+            return lh(t, "RAW", C * i + C, C * i)
+
+        def part(key, i, k=1):
+            return lf(t, key, 20 * (i + k), 20 * i)
+
+        send_scales(t)
+        send_codes(t, 1)
+        for h in range(2):
+            a, z = CUT[h], CUT[h + 1]
+            mm(4 + h, up, A(n("qc"), a, z), A(n("qs"), a, z), z - a)
+        for b in range(4):
+            mm(b, E(b), qc, qs, C)
+        for h in range(2):
+            a, z = CUT[h], CUT[h + 1]
+            scalar1(lb(t, "F", z, a), A("ps%d" % (4 + h), 0, z - a), 0.0, ALU.is_gt)
+            act(lb(t, "F2", z, a), lb(t, "F", z, a))
+        for h in range(2):
+            a, z = CUT[h], CUT[h + 1]
+            two_at(lb(t, "M", z, a), F, A("nx16", a // 16, z // 16), lb(t, "F2", z, a), ALU.is_lt)
+
+        def own(b):
+            act(A(n("tp"), TW * b, TW * b + C), A("ps%d" % b, 0, C))
+
+        own(0)
+        scan(Cn, M, M, ALU.add, ALU.max)
+        sl = A(n("sl"), 0, 12)
+        for m in range(3):
+            j, acc = lb(t, "JS", C * m + C, C * m), lf(t, "ACC", m + 1, m)
+            kb = A("kb", m, m + 1)
+            op("s", lambda q, j=j, acc=acc, kb=kb: q.activation(j[0], Cn[0], ACT.Sign, bias=kb[0], scale=-1.0, accum_out=acc[0]),
+               [j, acc], [Cn, kb])
+        for m in (3, 4):
+            scalar1(A("jv", AW * (m - 3), AW * (m - 3) + C), Cn, A("jw", m, m + 1), ALU.is_le, 2.0, ALU.mult)
+        for m in (3, 4):
+            j, acc = A("jv", AW * (m - 3), AW * (m - 3) + C + 1), lf(t, "ACC", m + 1, m)
+            op("v", lambda q, j=j, acc=acc: q.tensor_reduce(acc[0], j[0], AxisListType.X, ALU.add), [acc], [j])
+        scalar1(A(n("sl"), 0, 5), lf(t, "ACC", 5), 0.5, ALU.mult, C / 2.0, ALU.add)
+        pick("v", lh(t, "NXA", K), A("nxf", 0, AW), A(n("sl"), 0, 5))
+        scalar1(A(n("sl"), 10, 12), lb(t, "C", C, C - 2), float(K), ALU.min, 2.0, ALU.mult)
+        diagonal(lh(t, "NXR", K), lh(t, "NXA", K), K)
+        scalar1(A(n("sl"), 5, 10), lh(t, "NXR", K, 15, 16), offp, ALU.subtract)
+        send(A(n("ll"), 0, 12)[0], sl[0], n("rl"), where, [sl], n_out)
+        if t == 0:
+            for b in range(4):
+                iota_f(A("ta", AW * b + C, AW * b + AW), 0, AW - C, 0)
+            iota_f(A("wd", 0, 176), 0, 176, 0)
+            iota_f(A("o2", 0, 40), 0, 40, 0)
+
+        own(1)
+        own(2)
+        own(3)
+        if t == 0:
+            pf, io = A("pvf", 0, C), A("iotaf", 0, C)
+            op("v", lambda q: q.tensor_copy(pf[0].indirect(nx16[0]), io[0]), [pf], [io, nx16])
+        two_at(B, F, nx16, F2, ALU.is_gt)
+        if t == 0:
+            diagonal(A("pvr", 0, C), pf, C)
+        scan(CB, B, B, ALU.add, ALU.add)
+        if t == 0:
+            scalar1(pv16, A("pvr", 15, C, 16), offp, ALU.subtract)
+            scalar1(pvw, A("pvr", 15, C, 16), offp, ALU.subtract)
+        diagonal(raw(4), F, C)
+        pick("s", I, B, pv16)
+        pick("s", CBP, CB, pv16)
+        diagonal(raw(2), B, C)
+        diagonal(raw(0), CB, C)
+        if t == 0:
+            two(A("cj", 0, 20), jw, nxw, ALU.subtract)
+            two(A("cj", 20, 40), jw, pvw, ALU.subtract)
+            two(A("cj", 40, 60), pvw, nxw, ALU.subtract)
+        diagonal(raw(3), I, C)
+        diagonal(raw(1), CBP, C)
+        scalar1(W5, lh(t, "RAW", 5 * C, 15, 16), offp, ALU.subtract)
+        two(lf(t, "PR", 40), part("W5", 0, 2), part("W5", 2, 2), ALU.mult)
+        two(lf(t, "X60", 60), part("W5", 2, 3), A("cj", 0, 60), ALU.mult)
+        two(lf(t, "Z", 20), part("W5", 2), part("W5", 3), ALU.add)
+        two(KK, part("PR", 0), part("PR", 1), ALU.add)
+        two(part("KK", 1), part("PR", 0), part("PR", 1), ALU.add)
+        two(lf(t, "ZC", 20), lf(t, "Z", 20), A("cz", 0, 20), ALU.mult)
+        two(lf(t, "Y", 20), part("X60", 0), part("X60", 1), ALU.add)
+        two(lf(t, "Y2", 20), part("X60", 2), nxw, ALU.add)
+        two(part("DT", 1), KK, part("W5", 2), ALU.subtract)
+        two(part("DT", 0), KK, lf(t, "ZC", 20), ALU.add)
+        two(O2, lf(t, "Y", 20), lf(t, "Y2", 20), ALU.add)
+
+        for h in range(2):
+            a, z = CUT[h], CUT[h + 1]
+            for b in range(4):
+                bank = b if h else 4 + b
+                mm(bank, E(b), A(n("lc"), a, z), A(n("ls"), a, z), z - a)
+                act(A("ta", AW * b + a, AW * b + z), A("ps%d" % bank, 0, z - a))
+        for b in range(4):
+            pick("vvss"[b], A(n("at"), b, 4 * P2, 4), A("ta", AW * b, AW * b + AW), A(n("ll"), 0, 10))
+        ac, as_ = A(n("ac"), 0, P2), A(n("as"), 0, P2)
+        quant(ac, as_, A(n("at"), 0, 4 * P2))
+        for b in range(4):
+            mm(b, W(b), ac, as_, P2)
+        copy(lf(t, "NP", 2), A(n("ll"), 10, 12))
+        scalar1(lf(t, "U", 40), lf(t, "KK", 40), lf(t, "NP", 2, 1), ALU.is_le)
+        two(lf(t, "MM", 40), lf(t, "U", 40), lf(t, "DT", 40), ALU.mult)
+        two(lf(t, "RR", 40), lf(t, "MM", 40), A("o2", 0, 40), ALU.add)
+        copy(A(n("hk"), 0, 40), lf(t, "RR", 40))
+        for b in range(4):
+            out, z = A(n("ht"), b, 4 * P2, 4), A("ps%d" % b, 0, P2)
+            if b < 2:
+                act(out, z, 0.03125)
+            else:
+                scalar1(out, z, 0.03125, ALU.mult)
+        hc, hs = A(n("hc"), 0, P2), A(n("hs"), 0, P2)
+        quant(hc, hs, A(n("ht"), 0, 4 * P2))
+        mm(6, up, hc, hs, P2)
+        hb = lf(t, "HB", C)
+        pick("s", hb, A("iotaf", 0, TW), A(n("hk"), 0, 20))
+        for b in range(4):
+            for i in range(2):
+                out, z = A(n("tp"), TW * b + C + i, TW * b + TW, 2), A("ps%d" % b, K * i, K * i + K)
+                if b < 2:
+                    act(out, z, 0.03125)
+                else:
+                    scalar1(out, z, 0.03125, ALU.mult)
+        act(lf(t, "PS", K), A("ps6", 0, K))
+        two(A("wd", 1, P2 + 1, 2), lf(t, "PS", K), A("ps6", K, P2), ALU.is_lt)
+        two(A("wd", 2, P2 + 1, 2), lf(t, "PS", K), A("ps6", K, P2), ALU.is_ge)
+        two_at(lh(t, "V", C), A("wd", 0, 176), A(n("hk"), 20, 40), hb, ALU.add)
+        diagonal(lh(t, "VR", C), lh(t, "V", C), C)
+        scalar1(A(n("h"), 0, 20), lh(t, "VR", C, 15, 16), offp, ALU.subtract)
+        for h in range(2):
+            a, z = CUT[h], CUT[h + 1]
+            for b in range(4):
+                pick(("vvss", "vsss")[h][b], A("x%d" % (t + 1), 4 * a + b, 4 * z, 4), A(n("tp"), TW * b, TW * b + TW),
+                     A(n("h"), a // 16, z // 16))
+            state_codes(t + 1, h)
+            if h == 0 and t + 1 < R:
+                send_codes(t + 1, 0)
+            if h == 0 and t + 1 == R:
+                quant(A("vc", 0, 128), A("vs", 0, 128), A("vt", 0, 512))
+                dma("y", T.oc[:, 0:4 * z], U8(A("qc3", 0, z)), [], [A("qc3", 0, z)])
+
+    for h in range(2):
+        a, z = CUT[h], CUT[h + 1]
+        mm(4 + h, (A("vc", 0, 128), A("vs", 0, 128)), A("qc3", a, z), A("qs3", a, z), z - a)
+    copy(A("ott", 0, C), lh(R - 1, "V", C))
+    act(A("yt", 0, CUT[1]), A("ps4", 0, CUT[1]))
+    dma("s", T.y[:, 0:CUT[1]], A("yt", 0, CUT[1])[0], [], [A("yt", 0, CUT[1])])
+    dma("y", T.oc[:, 4 * CUT[1]:4 * C], U8(A("qc3", CUT[1], C)), [], [A("qc3", CUT[1], C)])
+    for k in range(4):
+        dma("y", T.osc[4 * k:4 * k + 4, :], T.qs3[32 * k:32 * k + 4, 0:C], [], [A("qs3", 0, C)])
+    act(A("yt", CUT[1], C), A("ps5", 0, C - CUT[1]))
+    dma("s", T.y[:, CUT[1]:C], A("yt", CUT[1], C)[0], [], [A("yt", CUT[1], C)])
+    dma("y", T.ot[:, :], T.ott[0:128:16, 0:C], [], [A("ott", 0, C)])
+    close()

@@ -5,11 +5,14 @@ ALU = AluOpType
 ACT = ActivationFunctionType
 C, K, R, N = 320, 80, 3, 4
 CUT = (0, 192, C)
+DEAL = (("s", 0, 104), ("v", 104, 192), ("s", 192, 272), ("v", 272, C))
 P2 = 2 * K
 TW = C + P2
 AW = C + 16
 OFF, BIG = 1024.0, 4096.0
 HALF = "float16"
+SKIP = 16
+NP = C // 2 - SKIP
 
 
 def _layout(sizes, align):
@@ -20,31 +23,27 @@ def _layout(sizes, align):
     return at, pos
 
 
-LB, LBW = _layout([("F", C), ("F2", C), ("M", C), ("C", C), ("B", C), ("CB", C), ("CBP", C), ("I", C), ("JS", 3 * C)], 16)
-LH, LHW = _layout([("NXA", K), ("NXR", K), ("RAW", 5 * C), ("V", C), ("VR", C)], 16)
-LF, LFW = _layout([("HB", C), ("ACC", 8), ("PS", K), ("W5", 100), ("PR", 40), ("KK", 40), ("X60", 60), ("Y", 20), ("Y2", 20),
-                   ("Z", 20), ("ZC", 20), ("DT", 40), ("U", 40), ("MM", 40), ("RR", 40), ("NP", 2)], 8)
+LB, LBW = _layout([("Z", NP), ("M", C), ("PAD", 16), ("B", C), ("F", C), ("G", C), ("FN", C), ("E", C + 2), ("NN", C), ("EP", C),
+                   ("JS", C), ("JV", 3 * NP), ("WD", 2 * C), ("MW", 32), ("M0", 32), ("M1", 32), ("D16", C), ("D4", C)], 16)
+LH, LHW = _layout([("NXA", K), ("NXR", K), ("RAW", 3 * C), ("SC", 3 * NP), ("V", C), ("VR", C)], 16)
+LF, LFW = _layout([("HB", C), ("ACC", 2), ("PS", K), ("Q", 160), ("S1", 80), ("ZY", 40), ("DU", 40), ("RR", 40), ("TH", 1), ("JW", 20),
+                   ("PVW", 20), ("KB", 2), ("LO", 3), ("HI", 3), ("INIT", 3), ("OFFP", 2), ("C0", 2), ("O4", 1), ("C4", 1)], 8)
+LI, LIW = _layout([("J0", 20), ("MV", 64), ("PI", 20), ("PJ", 20), ("PT", 1), ("MD", 32), ("W", 60), ("P", 60), ("CJ", 60)], 8)
+LU, LUW = _layout([("UL", 8), ("PJ", 20), ("PV", 20), ("SN", 6), ("IDX", 20), ("H4", 80)], 8)
 
 X4 = "float8_e4m3fn_x4"
 SCRATCH = {
-    "iotaf": ("sbuf", [128, TW], "float32"), "mi": ("sbuf", [128, 16], "int32"), "mj": ("sbuf", [128, 16], "int32"),
-    "m0": ("sbuf", [128, 16], HALF), "m1": ("sbuf", [128, 16], HALF), "dmask": ("sbuf", [128, C], HALF),
-    "pi": ("sbuf", [128, 20], "int32"), "pj": ("sbuf", [128, 20], "int32"), "j0": ("sbuf", [128, 20], "int32"),
-    "jw": ("sbuf", [128, 20], "float32"), "offp": ("sbuf", [128, 2], "float32"), "kb": ("sbuf", [128, 8], "float32"),
-    "uli": ("sbuf", [128, 8], "int32"), "ul": ("sbuf", [128, 8], "uint16"),
-    "ones": ("sbuf", [128, 128], "bfloat16"), "eb": ("sbuf", [128, 516], "bfloat16"),
+    "iotaf": ("sbuf", [128, 2 * C], "float32"), "ones": ("sbuf", [128, 128], "bfloat16"), "eb": ("sbuf", [128, 516], "bfloat16"),
     "ec": ("sbuf", [128, 512], X4), "es": ("sbuf", [128, 512], "uint8"),
     "ut": ("sbuf", [128, 512], "bfloat16"), "uc": ("sbuf", [128, 128], X4), "us": ("sbuf", [128, 128], "uint8"),
     "upc": ("sbuf", [128, 128], X4), "ups": ("sbuf", [128, 128], "uint8"),
     "vt": ("sbuf", [128, 512], "bfloat16"), "vc": ("sbuf", [128, 128], X4), "vs": ("sbuf", [128, 128], "uint8"),
     "lwc": ("sbuf", [128, 512], X4), "lws": ("sbuf", [128, 512], "uint8"),
-    "nxi": ("sbuf", [128, 20], "int32"), "nx16": ("sbuf", [128, 20], "uint16"), "nxw": ("sbuf", [128, 20], "float32"),
-    "nxf": ("sbuf", [128, AW], "float32"), "pvf": ("sbuf", [128, C], "float32"), "pvr": ("sbuf", [128, C], "float32"),
-    "pvw": ("sbuf", [128, 20], "float32"), "pv16": ("sbuf", [128, 20], "uint16"), "cj": ("sbuf", [128, 60], "float32"),
-    "cz": ("sbuf", [128, 20], "float32"),
-    "ta": ("sbuf", [128, 4 * AW], "bfloat16"), "wd": ("sbuf", [128, 176], "bfloat16"),
-    "jv": ("sbuf", [128, 2 * AW], "bfloat16"), "o2": ("sbuf", [128, 40], "float32"),
-    "lb": ("sbuf", [128, R * LBW], "bfloat16"), "lf": ("sbuf", [128, R * LFW], "float32"), "lh": ("sbuf", [128, R * LHW], HALF),
+    "nxi": ("sbuf", [128, 20], "int32"), "nx16": ("sbuf", [128, 20], "uint16"), "lnx": ("sbuf", [128, 20], "uint16"),
+    "nxf": ("sbuf", [128, AW], "float32"), "pvf": ("sbuf", [128, C], "float32"), "pvr": ("sbuf", [128, C], HALF),
+    "ta": ("sbuf", [128, 4 * AW], "bfloat16"),
+    "lb": ("sbuf", [128, LBW], "bfloat16"), "lf": ("sbuf", [128, LFW], "float32"), "lh": ("sbuf", [128, LHW], HALF),
+    "li": ("sbuf", [128, LIW], "int32"), "lu": ("sbuf", [128, LUW], "uint16"),
     "yt": ("sbuf", [128, C], "float32"), "ott": ("sbuf", [128, C], "float32"),
 }
 for _t in range(R + 1):
@@ -58,17 +57,14 @@ for _t in range(R):
     SCRATCH["at%d" % _t] = ("sbuf", [128, 4 * P2], "bfloat16")
     SCRATCH["ac%d" % _t] = ("sbuf", [128, P2], X4)
     SCRATCH["as%d" % _t] = ("sbuf", [128, P2], "uint8")
-    SCRATCH["ht%d" % _t] = ("sbuf", [128, 4 * P2], "bfloat16")
     SCRATCH["hc%d" % _t] = ("sbuf", [128, P2], X4)
     SCRATCH["hs%d" % _t] = ("sbuf", [128, P2], "uint8")
-    SCRATCH["sl%d" % _t] = ("sbuf", [128, 12], "uint16")
-    SCRATCH["ll%d" % _t] = ("sbuf", [128, 12], "uint16")
-    SCRATCH["hk%d" % _t] = ("sbuf", [128, 40], "uint16")
-    SCRATCH["h%d" % _t] = ("sbuf", [128, 20], "uint16")
+    SCRATCH["sl%d" % _t] = ("sbuf", [128, 6], "uint16")
+    SCRATCH["ll%d" % _t] = ("sbuf", [128, 6], "uint16")
 for _b in range(8):
     SCRATCH["ps%d" % _b] = ("psum", [128, 512], "float32")
 
-SEMAPHORES = (["cv", "cs", "ct", "cg", "loc"] + ["d%d" % i for i in range(20)]
+SEMAPHORES = (["cv", "cs", "ct", "cg", "loc", "rn"] + ["d%d" % i for i in range(20)]
               + [s + "%d" % t for t in range(R) for s in ("ra", "rb", "rs", "rl")])
 
 
@@ -158,19 +154,12 @@ def rank_program(g, core, T, topo):
     n_out, n_in = len(topo.engines(core, dst)), len(topo.engines(src, core))
 
     def A(name, a, b, step=1):
-        return (T[name][:, a:b:step] if step > 1 else T[name][:, a:b], name, _cols(a, b, step))
+        return (T[name][:, a:b:step] if step > 1 else T[name][:, a:b], name, 1 if name.startswith("ps") else _cols(a, b, step))
 
-    def lb(t, key, n, a=0, step=1):
-        o = t * LBW + LB[key]
-        return A("lb", o + a, o + n, step)
+    def part_of(name, at):
+        return lambda key, a, b, step=1: A(name, at[key] + a, at[key] + b, step)
 
-    def lf(t, key, n, a=0, step=1):
-        o = t * LFW + LF[key]
-        return A("lf", o + a, o + n, step)
-
-    def lh(t, key, n, a=0, step=1):
-        o = t * LHW + LH[key]
-        return A("lh", o + a, o + n, step)
+    lb, lh, lf, li, lu = part_of("lb", LB), part_of("lh", LH), part_of("lf", LF), part_of("li", LI), part_of("lu", LU)
 
     def U8(acc):
         return acc[0].bitcast(dt.uint8)
@@ -194,12 +183,12 @@ def rank_program(g, core, T, topo):
             op("s", lambda e: e.activation(out[0], win[0].indirect(off[0]), ACT.Copy), [out], [win, off])
 
     def scalar1(out, in0, s1, op0, s2=None, op1=None):
-        reads = [in0] + ([s1] if isinstance(s1, tuple) else [])
-        a1 = s1[0] if isinstance(s1, tuple) else s1
+        cols = [s for s in (s1, s2) if isinstance(s, tuple)]
+        a1, a2 = [s[0] if isinstance(s, tuple) else s for s in (s1, s2)]
         if op1 is None:
-            op("v", lambda q: q.tensor_scalar(out[0], in0[0], a1, None, op0), [out], reads)
+            op("v", lambda q: q.tensor_scalar(out[0], in0[0], a1, None, op0), [out], [in0] + cols)
         else:
-            op("v", lambda q: q.tensor_scalar(out[0], in0[0], a1, s2, op0, op1), [out], reads)
+            op("v", lambda q: q.tensor_scalar(out[0], in0[0], a1, a2, op0, op1), [out], [in0] + cols)
 
     def two(out, in0, in1, o):
         op("v", lambda q: q.tensor_tensor(out[0], in0[0], in1[0], o), [out], [in0, in1])
@@ -207,11 +196,13 @@ def rank_program(g, core, T, topo):
     def two_at(out, win, off, in1, o):
         op("v", lambda q: q.tensor_tensor(out[0], win[0].indirect(off[0]), in1[0], o), [out], [win, off, in1])
 
-    def scan(out, d0, d1, op0, op1):
-        op("v", lambda q: q.tensor_tensor_scan(out[0], d0[0], d1[0], 0.0, op0, op1), [out], [d0, d1])
+    def scan(out, d0, d1, op0, op1, first=0.0):
+        col = isinstance(first, tuple)
+        op("v", lambda q: q.tensor_tensor_scan(out[0], d0[0], d1[0], first[0] if col else first, op0, op1), [out],
+           [d0, d1] + ([first] if col else []))
 
-    def diagonal(raw, rows, n):
-        scan(raw, A("dmask", 0, n), rows, ALU.add, ALU.max)
+    def diagonal(raw, rows, n, mask="D16"):
+        scan(raw, lb(mask, 0, n), rows, ALU.add, ALU.max)
 
     def quant(c, s, tile):
         op("v", lambda q: q.quantize_mx(c[0], s[0], tile[0]), [c, s], [tile])
@@ -220,21 +211,29 @@ def rank_program(g, core, T, topo):
         out = A("ps%d" % bank, 0, n)
         op("t", lambda q: q.matmul_mx(out[0], w[0][0], w[1][0], xc[0], xs[0], True, True), [out], [w[0], w[1], xc, xs])
 
-    def act(out, in_, scale=None):
-        if scale is None:
-            op("s", lambda q: q.activation(out[0], in_[0], ACT.Copy), [out], [in_])
-        else:
+    def act(out, in_, scale=None, bias=None):
+        if bias is not None:
+            op("s", lambda q: q.activation(out[0], in_[0], ACT.Identity, bias=bias, scale=scale), [out], [in_])
+        elif scale is not None:
             op("s", lambda q: q.activation(out[0], in_[0], ACT.Copy, scale=scale), [out], [in_])
+        else:
+            op("s", lambda q: q.activation(out[0], in_[0], ACT.Copy), [out], [in_])
 
-    def load(q, name, a, b, ap):
+    def const(out, n, value):
+        act(out, A("ones", 0, n), value)
+
+    def load(q, name, a, b, ap, after=()):
         w = A(name, a, b)
-        dma(q, w[0], ap, [w], [])
+        dma(q, w[0], ap, [w], list(after))
 
     def iota(out, pattern, base, ch):
         op("g", lambda q: q.iota(out[0], pattern, base, ch), [out], [])
 
-    def iota_f(out, step, n, base):
-        op("g", lambda q: q.iota(out[0], [[step, n]], base, 0, allow_small_or_imprecise_dtypes=True), [out], [])
+    def iota_f(out, pattern, base):
+        op("g", lambda q: q.iota(out[0], pattern, base, 0, allow_small_or_imprecise_dtypes=True), [out], [])
+
+    def codes(name, a, b):
+        return A(name.replace("_", "c"), a, b), A(name.replace("_", "s"), a, b)
 
     def state_codes(t, h):
         a, b = CUT[h], CUT[h + 1]
@@ -254,203 +253,205 @@ def rank_program(g, core, T, topo):
     load("y", "x0", 4 * CUT[1], 4 * C, T.x[:, 4 * CUT[1]:4 * C])
     w = A("lwc", 0, 512)
     dma("y", U8(w), T.wc[:, :], [w], [])
-    load("s", "lws", 0, 512, T.ws[:, :])
-    load("y", "vt", 0, 512, T.v[:, :])
+    load("y", "lws", 0, 512, T.ws[:, :])
+    lands([A("lnx", 0, 20)], "rn", n_in)
     for t in range(R):
         lands([A("lc%d" % t, 0, CUT[1])], "ra%d" % t, n_in)
         lands([A("lc%d" % t, CUT[1], C)], "rb%d" % t, n_in)
         lands([A("ls%d" % t, 0, C)], "rs%d" % t, n_in)
-        lands([A("ll%d" % t, 0, 12)], "rl%d" % t, n_in)
+        lands([A("ll%d" % t, 0, 6)], "rl%d" % t, n_in)
 
+    nx16, pv16, nxw, jw, pvw = A("nx16", 0, 20), lu("PV", 0, 20), lf("Q", 121, 160, 2), lf("JW", 0, 20), lf("PVW", 0, 20)
+    offp, io = lf("OFFP", 0, 1), A("iotaf", 0, C)
     fill(A("ones", 0, 128), 1.0)
     fill(A("eb", 0, 516), 0.0)
-    iota(A("uli", 0, 8), [[16, 8]], 0, 0)
-    iota(A("mi", 0, 16), [[1, 16]], 128, -1)
-    iota(A("pi", 0, 20), [[0, 20]], 0, 1)
-    iota(A("j0", 0, 20), [[16, 20]], 0, 0)
+    iota(li("J0", 0, 20), [[16, 20]], 0, 0)
+    iota(li("MV", 0, 64), [[1, 64]], 128, -1)
+    iota(li("PI", 0, 20), [[0, 20]], 0, 1)
     e, o = A("eb", 3, 515, 4), A("ones", 0, 128)
     op("g", lambda q: q.affine_select(e[0], o[0], [[-1, 128]], ALU.is_equal, 0.0, 0, 1), [e], [o])
-    iota_f(A("iotaf", 0, TW), 1, TW, 0)
-    for b in range(2):
-        iota_f(A("jv", AW * b + C, AW * b + C + 8), 0, 8, -C)
-    copy(A("ul", 0, 8), A("uli", 0, 8))
-    scalar1(A("mj", 0, 16), A("mi", 0, 16), 15, ALU.bitwise_and)
-    scalar1(A("pj", 0, 20), A("pi", 0, 20), 15, ALU.bitwise_and)
-    scalar1(A("m0", 0, 16), A("mj", 0, 16), 0.0, ALU.is_equal, -BIG, ALU.mult)
-    scalar1(A("m1", 0, 16), A("mj", 0, 16), 1.0, ALU.is_equal, OFF, ALU.mult)
-    two(A("jw", 0, 20), A("j0", 0, 20), A("pj", 0, 20), ALU.add)
-    two(A("dmask", 0, 16), A("m0", 0, 16), A("m1", 0, 16), ALU.add)
-    scalar1(A("offp", 0, 2), A("pj", 0, 2), 14.5, ALU.is_lt, OFF, ALU.mult)
+    iota_f(io, [[1, C]], 0)
+    const(lb("Z", 0, 128), 128, 0.0)
+    const(lb("Z", 128, NP), NP - 128, 0.0)
+    const(lb("PAD", 0, 16), 16, 0.0)
+    const(lf("Q", 0, 160, 2), 80, 0.0)
+    const(lf("DU", 0, 40, 2), 20, -BIG)
+    const(A("ta", C, 4 * AW, AW), 4, 0.0)
+    const(A("nxf", C, C + 1), 1, float(C))
+    copy(lu("UL", 0, 8), li("J0", 0, 8))
+    scalar1(li("MD", 0, 16), li("MV", 0, 16), 15, ALU.bitwise_and)
+    scalar1(li("MD", 16, 32), li("MV", 3, 64, 4), 2, ALU.arith_shift_right, 3, ALU.bitwise_and)
+    scalar1(li("PJ", 0, 20), li("PI", 0, 20), 15, ALU.bitwise_and)
+    scalar1(lb("M0", 0, 32), li("MD", 0, 32), 0.0, ALU.is_equal, -BIG, ALU.mult)
+    scalar1(lb("M1", 0, 32), li("MD", 0, 32), 1.0, ALU.is_equal, OFF, ALU.mult)
+    copy(lu("PJ", 0, 20), li("PJ", 0, 20))
+    two(jw, li("J0", 0, 20), li("PJ", 0, 20), ALU.add)
+    two(lb("MW", 0, 32), lb("M0", 0, 32), lb("M1", 0, 32), ALU.add)
+    scalar1(li("PT", 0, 1), li("PI", 0, 1), 3, ALU.bitwise_and)
     for b in range(4):
         quant(E(b)[0], E(b)[1], A("eb", 3 - b, 515 - b))
-        copy(A("dmask", 16 << b, 32 << b), A("dmask", 0, 16 << b))
-    fill(A("nxf", C, AW), float(C))
-    copy(A("dmask", 256, C), A("dmask", 0, C - 256))
-    scalar1(A("kb", 0, 5), A("jw", 0, 5), 0.5, ALU.add)
-    copy(A("nx16", 0, 20), A("nxi", 0, 20))
-    copy(A("nxw", 0, 20), A("nxi", 0, 20))
-    scalar1(A("cz", 0, 20), A("jw", 0, 20), -1.0, ALU.mult, C - 2.0, ALU.add)
+    scalar1(lf("OFFP", 0, 2), lb("MW", 15, 32, 16), -1.0, ALU.is_gt, OFF, ALU.mult)
+    scalar1(lf("O4", 0, 1), lb("MW", 31, 32), -1.0, ALU.is_gt, -4 * OFF, ALU.mult)
+    act(lf("KB", 0, 2), lf("JW", 0, 2), 2.0, 1.0)
+    act(lf("LO", 0, 3), lf("JW", 2, 5), 2.0)
+    act(lf("HI", 0, 3), lf("JW", 2, 5), 2.0, 2.0)
+    act(lf("INIT", 0, 3), lf("JW", 2, 5), 2.0 * NP, float(C))
+    pick("s", lb("D16", 0, C), lb("MW", 0, 16), lu("PJ", 0, 20))
+    copy(nx16, A("nxi", 0, 20))
+    send(A("lnx", 0, 20)[0], nx16[0], "rn", where, [nx16], n_out)
+    copy(nxw, A("nxi", 0, 20))
+    two(lf("C4", 0, 1), lf("O4", 0, 1), li("PT", 0, 1), ALU.add)
+    for i in range(2):
+        act(lf("C0", i, i + 1), offp, 2.0, 2.0 * C + i)
     quant(A("uc", 0, 128), A("us", 0, 128), A("ut", 0, 512))
-    up, ic_, ul = (A("upc", 0, 128), A("ups", 0, 128)), A("uc", 0, 128), A("ul", 0, 8)
+    up, ic_, ul = (A("upc", 0, 128), A("ups", 0, 128)), A("uc", 0, 128), lu("UL", 0, 8)
     op("v", lambda q: q.tensor_copy(up[0][0].bitcast(dt.uint32), ic_[0].bitcast(dt.uint32).indirect(ul[0])), [up[0]], [ic_, ul])
     pick("s", up[1], A("us", 0, 128), ul)
+    pick("s", lb("D4", 0, C), lb("MW", 16, 32), lu("PJ", 0, 20))
     state_codes(0, 0)
     send_codes(0, 0)
+    mm(4, up, *codes("q_0", 0, CUT[1]), CUT[1])
     state_codes(0, 1)
-    pick("s", A("nxf", 0, C), A("iotaf", 0, C), A("nx16", 0, 20))
-    offp, nx16, pv16, nxw, jw, pvw = A("offp", 0, 1), A("nx16", 0, 20), A("pv16", 0, 20), A("nxw", 0, 20), A("jw", 0, 20), A("pvw", 0, 20)
+
+    F, G, FN, NN, EP = lb("F", 0, C), lb("G", 0, C), lb("FN", 0, C), lb("NN", 0, C), lb("EP", 0, C)
+
+    def raw(i, k=1, last=False):
+        return lh("RAW", C * i + 15, C * (i + k), 16) if last else lh("RAW", C * i, C * (i + k))
 
     for t in range(R):
         n = lambda s: "%s%d" % (s, t)
-        qc, qs = A(n("qc"), 0, C), A(n("qs"), 0, C)
-        F, F2, M, Cn, B = lb(t, "F", C), lb(t, "F2", C), lb(t, "M", C), lb(t, "C", C), lb(t, "B", C)
-        CB, CBP, I, W5, KK, O2 = lb(t, "CB", C), lb(t, "CBP", C), lb(t, "I", C), lf(t, "W5", 100), lf(t, "KK", 20), A("o2", 0, 20)
-
-        def raw(i):
-            return lh(t, "RAW", C * i + C, C * i)
-
-        def part(key, i, k=1):
-            return lf(t, key, 20 * (i + k), 20 * i)
-
+        tp = A(n("tp"), 0, 4 * TW)
         send_scales(t)
         send_codes(t, 1)
-        for h in range(2):
-            a, z = CUT[h], CUT[h + 1]
-            mm(4 + h, up, A(n("qc"), a, z), A(n("qs"), a, z), z - a)
+        mm(5, up, *codes(n("q_"), CUT[1], C), C - CUT[1])
         for b in range(4):
-            mm(b, E(b), qc, qs, C)
+            mm(b, E(b), *codes(n("q_"), 0, C), C)
         for h in range(2):
             a, z = CUT[h], CUT[h + 1]
-            scalar1(lb(t, "F", z, a), A("ps%d" % (4 + h), 0, z - a), 0.0, ALU.is_gt)
-            act(lb(t, "F2", z, a), lb(t, "F", z, a))
-        for h in range(2):
-            a, z = CUT[h], CUT[h + 1]
-            two_at(lb(t, "M", z, a), F, A("nx16", a // 16, z // 16), lb(t, "F2", z, a), ALU.is_lt)
-
-        def own(b):
-            act(A(n("tp"), TW * b, TW * b + C), A("ps%d" % b, 0, C))
-
-        own(0)
-        scan(Cn, M, M, ALU.add, ALU.max)
-        sl = A(n("sl"), 0, 12)
+            scalar1(lb("F", a, z), A("ps%d" % (4 + h), 0, z - a), 0.0, ALU.is_gt)
+            scalar1(lb("G", a, z), A("ps%d" % (4 + h), 0, z - a), 0.0, ALU.is_gt, 1.0, ALU.subtract)
+        two_at(lb("M", 0, C), F, nx16, G, ALU.is_le)
+        pick("s", FN, F, nx16)
+        diagonal(raw(0), F, C)
+        scan(lb("E", 0, C + 2), lb("M", 0, C + 2), lb("M", -1, C + 1), ALU.add, ALU.add)
+        scan(lb("B", 0, C), FN, G, ALU.max, ALU.mult)
+        sl = A(n("sl"), 0, 6)
+        for m in range(2):
+            j, acc, kb, pairs = lb("JS", P2 * m, P2 * m + P2), lf("ACC", m, m + 1), lf("KB", m, m + 1), lb("E", 1, C, 2)
+            op("s", lambda q, j=j, acc=acc, kb=kb: q.activation(j[0], pairs[0], ACT.Sign, bias=kb[0], scale=-1.0, accum_out=acc[0]),
+               [j, acc], [pairs, kb])
         for m in range(3):
-            j, acc = lb(t, "JS", C * m + C, C * m), lf(t, "ACC", m + 1, m)
-            kb = A("kb", m, m + 1)
-            op("s", lambda q, j=j, acc=acc, kb=kb: q.activation(j[0], Cn[0], ACT.Sign, bias=kb[0], scale=-1.0, accum_out=acc[0]),
-               [j, acc], [Cn, kb])
-        for m in (3, 4):
-            scalar1(A("jv", AW * (m - 3), AW * (m - 3) + C), Cn, A("jw", m, m + 1), ALU.is_le, 2.0, ALU.mult)
-        for m in (3, 4):
-            j, acc = A("jv", AW * (m - 3), AW * (m - 3) + C + 1), lf(t, "ACC", m + 1, m)
-            op("v", lambda q, j=j, acc=acc: q.tensor_reduce(acc[0], j[0], AxisListType.X, ALU.add), [acc], [j])
-        scalar1(A(n("sl"), 0, 5), lf(t, "ACC", 5), 0.5, ALU.mult, C / 2.0, ALU.add)
-        pick("v", lh(t, "NXA", K), A("nxf", 0, AW), A(n("sl"), 0, 5))
-        scalar1(A(n("sl"), 10, 12), lb(t, "C", C, C - 2), float(K), ALU.min, 2.0, ALU.mult)
-        diagonal(lh(t, "NXR", K), lh(t, "NXA", K), K)
-        scalar1(A(n("sl"), 5, 10), lh(t, "NXR", K, 15, 16), offp, ALU.subtract)
-        send(A(n("ll"), 0, 12)[0], sl[0], n("rl"), where, [sl], n_out)
+            scalar1(lb("JV", NP * m, NP * m + NP), lb("E", 2 * SKIP + 1, C, 2), lf("LO", m, m + 1), ALU.max, lf("HI", m, m + 1), ALU.min)
+        for m in range(3):
+            scan(lh("SC", NP * m, NP * m + NP), lb("Z", 0, NP), lb("JV", NP * m, NP * m + NP), ALU.add, ALU.subtract, lf("INIT", m, m + 1))
+        scalar1(A(n("sl"), 5, 6), lb("E", C, C + 1), float(P2), ALU.min, 2.0, ALU.mult)
+        scalar1(A(n("sl"), 0, 2), lf("ACC", 0, 2), C / 2.0, ALU.add)
+        copy(A(n("sl"), 2, 5), lh("SC", NP - 1, 3 * NP, NP))
+        send(A(n("ll"), 0, 6)[0], sl[0], n("rl"), where, [sl], n_out)
+        scan(NN, lb("B", 0, C), lb("B", -1, C - 1), ALU.add, ALU.add, C / 2.0)
         if t == 0:
-            for b in range(4):
-                iota_f(A("ta", AW * b + C, AW * b + AW), 0, AW - C, 0)
-            iota_f(A("wd", 0, 176), 0, 176, 0)
-            iota_f(A("o2", 0, 40), 0, 40, 0)
-
-        own(1)
-        own(2)
-        own(3)
-        if t == 0:
-            pf, io = A("pvf", 0, C), A("iotaf", 0, C)
+            iota_f(A("iotaf", C, 2 * C), [[2, K], [0, 4]], C)
+            iota_f(lb("WD", 0, 2 * C), [[0, 2 * C]], 0)
+            pick("s", A("nxf", 0, C), io, A("lnx", 0, 20))
+            pf = A("pvf", 0, C)
             op("v", lambda q: q.tensor_copy(pf[0].indirect(nx16[0]), io[0]), [pf], [io, nx16])
-        two_at(B, F, nx16, F2, ALU.is_gt)
+        diagonal(raw(1), NN, C)
         if t == 0:
             diagonal(A("pvr", 0, C), pf, C)
-        scan(CB, B, B, ALU.add, ALU.add)
+        scalar1(li("W", 0, 40), raw(0, 2, True), -2.0, ALU.mult, lf("C0", 0, 1), ALU.add)
         if t == 0:
             scalar1(pv16, A("pvr", 15, C, 16), offp, ALU.subtract)
             scalar1(pvw, A("pvr", 15, C, 16), offp, ALU.subtract)
-        diagonal(raw(4), F, C)
-        pick("s", I, B, pv16)
-        pick("s", CBP, CB, pv16)
-        diagonal(raw(2), B, C)
-        diagonal(raw(0), CB, C)
-        if t == 0:
-            two(A("cj", 0, 20), jw, nxw, ALU.subtract)
-            two(A("cj", 20, 40), jw, pvw, ALU.subtract)
-            two(A("cj", 40, 60), pvw, nxw, ALU.subtract)
-        diagonal(raw(3), I, C)
-        diagonal(raw(1), CBP, C)
-        scalar1(W5, lh(t, "RAW", 5 * C, 15, 16), offp, ALU.subtract)
-        two(lf(t, "PR", 40), part("W5", 0, 2), part("W5", 2, 2), ALU.mult)
-        two(lf(t, "X60", 60), part("W5", 2, 3), A("cj", 0, 60), ALU.mult)
-        two(lf(t, "Z", 20), part("W5", 2), part("W5", 3), ALU.add)
-        two(KK, part("PR", 0), part("PR", 1), ALU.add)
-        two(part("KK", 1), part("PR", 0), part("PR", 1), ALU.add)
-        two(lf(t, "ZC", 20), lf(t, "Z", 20), A("cz", 0, 20), ALU.mult)
-        two(lf(t, "Y", 20), part("X60", 0), part("X60", 1), ALU.add)
-        two(lf(t, "Y2", 20), part("X60", 2), nxw, ALU.add)
-        two(part("DT", 1), KK, part("W5", 2), ALU.subtract)
-        two(part("DT", 0), KK, lf(t, "ZC", 20), ALU.add)
-        two(O2, lf(t, "Y", 20), lf(t, "Y2", 20), ALU.add)
 
-        for h in range(2):
+        def arrived(h):
             a, z = CUT[h], CUT[h + 1]
             for b in range(4):
-                bank = b if h else 4 + b
-                mm(bank, E(b), A(n("lc"), a, z), A(n("ls"), a, z), z - a)
-                act(A("ta", AW * b + a, AW * b + z), A("ps%d" % bank, 0, z - a))
+                mm(4 + b, E(b), *codes(n("l_"), a, z), z - a)
+                act(A("ta", AW * b + a, AW * b + z), A("ps%d" % (4 + b), 0, z - a))
+
+        def before():
+            pick("s", EP, NN, pv16)
+
+        for step in ((lambda: arrived(0), before) if t == 0 else (before, lambda: arrived(0))):
+            step()
+        arrived(1)
+        if t == 0:
+            two(li("CJ", 0, 20), pvw, nxw, ALU.subtract)
+            two(li("CJ", 20, 40), jw, nxw, ALU.subtract)
+            two(li("CJ", 40, 60), jw, pvw, ALU.subtract)
+        diagonal(raw(2), EP, C)
+        scalar1(li("W", 40, 60), raw(2, 1, True), -2.0, ALU.mult, lf("C0", 1, 2), ALU.add)
+        scalar1(li("P", 0, 60), li("W", 0, 60), 1, ALU.arith_shift_right, 1, ALU.bitwise_and)
+        two(lf("Q", 40, 120, 2), li("P", 20, 60), li("W", 20, 60), ALU.mult)
+        two(lf("Q", 1, 120, 2), li("P", 0, 60), li("CJ", 0, 60), ALU.mult)
+        two(lf("S1", 0, 80), lf("Q", 0, 80), lf("Q", 80, 160), ALU.add)
+        two(lf("ZY", 0, 40), lf("S1", 0, 40), lf("S1", 40, 80), ALU.add)
+
+        def parts(q, b, i, off):
+            pick(q, A(n("at"), 4 * i + b, 4 * P2, 8), A("ta", AW * b, AW * b + C + 1), off)
+
+        def own(b):
+            act(A(n("tp"), b, 4 * C, 4), A("ps%d" % b, 0, C))
+
+        ll, sn = A(n("ll"), 0, 5), lu("SN", 0, 5)
+        pick("v", lh("NXA", 0, K), A("nxf", 0, C + 1), ll)
+        if t == 0:
+            load("y", "vt", 0, 512, T.v[:, :], [ll])
+        parts("s", 2, 0, ll)
+        parts("s", 3, 0, ll)
+        parts("v", 0, 0, ll)
+        diagonal(lh("NXR", 0, K), lh("NXA", 0, K), K)
+        parts("v", 1, 0, ll)
+        scalar1(sn, lh("NXR", 15, K, 16), offp, ALU.subtract)
+        scalar1(lf("TH", 0, 1), A(n("ll"), 5, 6), C + 2.0, ALU.add)
         for b in range(4):
-            pick("vvss"[b], A(n("at"), b, 4 * P2, 4), A("ta", AW * b, AW * b + AW), A(n("ll"), 0, 10))
-        ac, as_ = A(n("ac"), 0, P2), A(n("as"), 0, P2)
-        quant(ac, as_, A(n("at"), 0, 4 * P2))
+            parts("vvss"[b], b, 1, sn)
+        quant(*codes(n("a_"), 0, P2), A(n("at"), 0, 4 * P2))
         for b in range(4):
-            mm(b, W(b), ac, as_, P2)
-        copy(lf(t, "NP", 2), A(n("ll"), 10, 12))
-        scalar1(lf(t, "U", 40), lf(t, "KK", 40), lf(t, "NP", 2, 1), ALU.is_le)
-        two(lf(t, "MM", 40), lf(t, "U", 40), lf(t, "DT", 40), ALU.mult)
-        two(lf(t, "RR", 40), lf(t, "MM", 40), A("o2", 0, 40), ALU.add)
-        copy(A(n("hk"), 0, 40), lf(t, "RR", 40))
+            mm(4 + b, W(b), *codes(n("a_"), 0, P2), P2)
+        own(0)
+        own(1)
+        scalar1(lf("DU", 1, 40, 2), lf("ZY", 0, 40, 2), lf("TH", 0, 1), ALU.is_ge, -BIG, ALU.mult)
+        scan(lf("RR", 0, 40), lf("DU", 0, 40), lf("ZY", 0, 40), ALU.add, ALU.max)
+        copy(lu("IDX", 0, 20), lf("RR", 1, 40, 2))
         for b in range(4):
-            out, z = A(n("ht"), b, 4 * P2, 4), A("ps%d" % b, 0, P2)
-            if b < 2:
+            out, z = A(n("tp"), 4 * C + b, 4 * TW, 4), A("ps%d" % (4 + b), 0, P2)
+            if b % 2 == 0:
                 act(out, z, 0.03125)
             else:
                 scalar1(out, z, 0.03125, ALU.mult)
-        hc, hs = A(n("hc"), 0, P2), A(n("hs"), 0, P2)
-        quant(hc, hs, A(n("ht"), 0, 4 * P2))
-        mm(6, up, hc, hs, P2)
-        hb = lf(t, "HB", C)
-        pick("s", hb, A("iotaf", 0, TW), A(n("hk"), 0, 20))
-        for b in range(4):
-            for i in range(2):
-                out, z = A(n("tp"), TW * b + C + i, TW * b + TW, 2), A("ps%d" % b, K * i, K * i + K)
-                if b < 2:
-                    act(out, z, 0.03125)
-                else:
-                    scalar1(out, z, 0.03125, ALU.mult)
-        act(lf(t, "PS", K), A("ps6", 0, K))
-        two(A("wd", 1, P2 + 1, 2), lf(t, "PS", K), A("ps6", K, P2), ALU.is_lt)
-        two(A("wd", 2, P2 + 1, 2), lf(t, "PS", K), A("ps6", K, P2), ALU.is_ge)
-        two_at(lh(t, "V", C), A("wd", 0, 176), A(n("hk"), 20, 40), hb, ALU.add)
-        diagonal(lh(t, "VR", C), lh(t, "V", C), C)
-        scalar1(A(n("h"), 0, 20), lh(t, "VR", C, 15, 16), offp, ALU.subtract)
+        quant(*codes(n("h_"), 0, P2), A(n("tp"), 4 * C, 4 * TW))
+        mm(0, up, *codes(n("h_"), 0, P2), P2)
+        pick("s", lf("HB", 0, C), A("iotaf", 0, 2 * C), lu("IDX", 0, 20))
+        own(2)
+        own(3)
+        if t + 1 == R:
+            quant(A("vc", 0, 128), A("vs", 0, 128), A("vt", 0, 512))
+        copy(lf("PS", 0, K), A("ps0", 0, P2, 2))
+        two(lb("WD", C + 2, 2 * C, 4), lf("PS", 0, K), A("ps0", 1, P2, 2), ALU.is_lt)
+        two(lb("WD", C + 3, 2 * C, 4), lf("PS", 0, K), A("ps0", 1, P2, 2), ALU.is_ge)
+        runs = [(CUT[h], CUT[h + 1]) for h in range(2)]
+        for a, z in runs:
+            two_at(lh("V", a, z), lb("WD", 0, 2 * C), lu("IDX", a // 16, z // 16), lf("HB", a, z), ALU.add)
+        for a, z in runs:
+            diagonal(lh("VR", a, z), lh("V", a, z), z - a, "D4")
+        for a, z in runs:
+            scalar1(lu("H4", a // 4, z // 4), lh("VR", a + 3, z, 4), 4.0, ALU.mult, lf("C4", 0, 1), ALU.add)
         for h in range(2):
-            a, z = CUT[h], CUT[h + 1]
-            for b in range(4):
-                pick(("vvss", "vsss")[h][b], A("x%d" % (t + 1), 4 * a + b, 4 * z, 4), A(n("tp"), TW * b, TW * b + TW),
-                     A(n("h"), a // 16, z // 16))
+            for q, a, z in DEAL[2 * h:2 * h + 2]:
+                pick(q, A("x%d" % (t + 1), 4 * a, 4 * z), tp, lu("H4", a // 4, z // 4))
             state_codes(t + 1, h)
             if h == 0 and t + 1 < R:
                 send_codes(t + 1, 0)
+                mm(4, up, *codes("q_%d" % (t + 1), 0, CUT[1]), CUT[1])
             if h == 0 and t + 1 == R:
-                quant(A("vc", 0, 128), A("vs", 0, 128), A("vt", 0, 512))
-                dma("y", T.oc[:, 0:4 * z], U8(A("qc3", 0, z)), [], [A("qc3", 0, z)])
+                mm(4, codes("v_", 0, 128), *codes("q_3", 0, CUT[1]), CUT[1])
+                dma("y", T.oc[:, 0:4 * CUT[1]], U8(A("qc3", 0, CUT[1])), [], [A("qc3", 0, CUT[1])])
 
-    for h in range(2):
-        a, z = CUT[h], CUT[h + 1]
-        mm(4 + h, (A("vc", 0, 128), A("vs", 0, 128)), A("qc3", a, z), A("qs3", a, z), z - a)
-    copy(A("ott", 0, C), lh(R - 1, "V", C))
+    mm(5, codes("v_", 0, 128), *codes("q_3", CUT[1], C), C - CUT[1])
     act(A("yt", 0, CUT[1]), A("ps4", 0, CUT[1]))
     dma("s", T.y[:, 0:CUT[1]], A("yt", 0, CUT[1])[0], [], [A("yt", 0, CUT[1])])
+    copy(A("ott", 0, C), lh("V", 0, C))
     dma("y", T.oc[:, 4 * CUT[1]:4 * C], U8(A("qc3", CUT[1], C)), [], [A("qc3", CUT[1], C)])
     for k in range(4):
         dma("y", T.osc[4 * k:4 * k + 4, :], T.qs3[32 * k:32 * k + 4, 0:C], [], [A("qs3", 0, C)])

@@ -5,7 +5,7 @@ ALU = AluOpType
 ACT = ActivationFunctionType
 C, K, R, N = 320, 80, 3, 4
 CUT = (0, 192, C)
-DEAL = (("s", 0, 104), ("v", 104, 192), ("s", 192, 272), ("v", 272, C))
+DEAL = ((("s", 0, 96), ("v", 96, 192), ("v", 192, 216)), (("s", 216, 296), ("v", 296, C)))
 P2 = 2 * K
 TW = C + P2
 AW = C + 16
@@ -268,9 +268,9 @@ def rank_program(g, core, T, topo):
     iota(li("J0", 0, 20), [[16, 20]], 0, 0)
     iota(li("MV", 0, 64), [[1, 64]], 128, -1)
     iota(li("PI", 0, 20), [[0, 20]], 0, 1)
+    iota_f(io, [[1, C]], 0)
     e, o = A("eb", 3, 515, 4), A("ones", 0, 128)
     op("g", lambda q: q.affine_select(e[0], o[0], [[-1, 128]], ALU.is_equal, 0.0, 0, 1), [e], [o])
-    iota_f(io, [[1, C]], 0)
     const(lb("Z", 0, 128), 128, 0.0)
     const(lb("Z", 128, NP), NP - 128, 0.0)
     const(lb("PAD", 0, 16), 16, 0.0)
@@ -288,8 +288,6 @@ def rank_program(g, core, T, topo):
     two(jw, li("J0", 0, 20), li("PJ", 0, 20), ALU.add)
     two(lb("MW", 0, 32), lb("M0", 0, 32), lb("M1", 0, 32), ALU.add)
     scalar1(li("PT", 0, 1), li("PI", 0, 1), 3, ALU.bitwise_and)
-    for b in range(4):
-        quant(E(b)[0], E(b)[1], A("eb", 3 - b, 515 - b))
     scalar1(lf("OFFP", 0, 2), lb("MW", 15, 32, 16), -1.0, ALU.is_gt, OFF, ALU.mult)
     scalar1(lf("O4", 0, 1), lb("MW", 31, 32), -1.0, ALU.is_gt, -4 * OFF, ALU.mult)
     act(lf("KB", 0, 2), lf("JW", 0, 2), 2.0, 1.0)
@@ -303,15 +301,23 @@ def rank_program(g, core, T, topo):
     two(lf("C4", 0, 1), lf("O4", 0, 1), li("PT", 0, 1), ALU.add)
     for i in range(2):
         act(lf("C0", i, i + 1), offp, 2.0, 2.0 * C + i)
+    pf = A("pvf", 0, C)
+    op("v", lambda q: q.tensor_copy(pf[0].indirect(nx16[0]), io[0]), [pf], [io, nx16])
     quant(A("uc", 0, 128), A("us", 0, 128), A("ut", 0, 512))
+    diagonal(A("pvr", 0, C), pf, C)
     up, ic_, ul = (A("upc", 0, 128), A("ups", 0, 128)), A("uc", 0, 128), lu("UL", 0, 8)
     op("v", lambda q: q.tensor_copy(up[0][0].bitcast(dt.uint32), ic_[0].bitcast(dt.uint32).indirect(ul[0])), [up[0]], [ic_, ul])
     pick("s", up[1], A("us", 0, 128), ul)
     pick("s", lb("D4", 0, C), lb("MW", 16, 32), lu("PJ", 0, 20))
+    scalar1(pv16, A("pvr", 15, C, 16), offp, ALU.subtract)
+    scalar1(pvw, A("pvr", 15, C, 16), offp, ALU.subtract)
     state_codes(0, 0)
     send_codes(0, 0)
     mm(4, up, *codes("q_0", 0, CUT[1]), CUT[1])
-    state_codes(0, 1)
+    for b in range(4):
+        quant(E(b)[0], E(b)[1], A("eb", 3 - b, 515 - b))
+        if b == 1:
+            state_codes(0, 1)
 
     F, G, FN, NN, EP = lb("F", 0, C), lb("G", 0, C), lb("FN", 0, C), lb("NN", 0, C), lb("EP", 0, C)
 
@@ -330,7 +336,9 @@ def rank_program(g, core, T, topo):
             a, z = CUT[h], CUT[h + 1]
             scalar1(lb("F", a, z), A("ps%d" % (4 + h), 0, z - a), 0.0, ALU.is_gt)
             scalar1(lb("G", a, z), A("ps%d" % (4 + h), 0, z - a), 0.0, ALU.is_gt, 1.0, ALU.subtract)
-        two_at(lb("M", 0, C), F, nx16, G, ALU.is_le)
+        for h in range(2):
+            a, z = CUT[h], CUT[h + 1]
+            two_at(lb("M", a, z), F, A("nx16", a // 16, z // 16), lb("G", a, z), ALU.is_le)
         pick("s", FN, F, nx16)
         diagonal(raw(0), F, C)
         scan(lb("E", 0, C + 2), lb("M", 0, C + 2), lb("M", -1, C + 1), ALU.add, ALU.add)
@@ -345,47 +353,30 @@ def rank_program(g, core, T, topo):
         for m in range(3):
             scan(lh("SC", NP * m, NP * m + NP), lb("Z", 0, NP), lb("JV", NP * m, NP * m + NP), ALU.add, ALU.subtract, lf("INIT", m, m + 1))
         scalar1(A(n("sl"), 5, 6), lb("E", C, C + 1), float(P2), ALU.min, 2.0, ALU.mult)
-        scalar1(A(n("sl"), 0, 2), lf("ACC", 0, 2), C / 2.0, ALU.add)
-        copy(A(n("sl"), 2, 5), lh("SC", NP - 1, 3 * NP, NP))
-        send(A(n("ll"), 0, 6)[0], sl[0], n("rl"), where, [sl], n_out)
         scan(NN, lb("B", 0, C), lb("B", -1, C - 1), ALU.add, ALU.add, C / 2.0)
+        copy(A(n("sl"), 2, 5), lh("SC", NP - 1, 3 * NP, NP))
+        scalar1(A(n("sl"), 0, 2), lf("ACC", 0, 2), C / 2.0, ALU.add)
+        send(A(n("ll"), 0, 6)[0], sl[0], n("rl"), where, [sl], n_out)
+        pick("s", EP, NN, pv16)
+        diagonal(raw(1), NN, C)
         if t == 0:
             iota_f(A("iotaf", C, 2 * C), [[2, K], [0, 4]], C)
             iota_f(lb("WD", 0, 2 * C), [[0, 2 * C]], 0)
-            pick("s", A("nxf", 0, C), io, A("lnx", 0, 20))
-            pf = A("pvf", 0, C)
-            op("v", lambda q: q.tensor_copy(pf[0].indirect(nx16[0]), io[0]), [pf], [io, nx16])
-        diagonal(raw(1), NN, C)
-        if t == 0:
-            diagonal(A("pvr", 0, C), pf, C)
+            two(li("CJ", 0, 20), pvw, nxw, ALU.subtract)
+            two(li("CJ", 20, 40), jw, nxw, ALU.subtract)
+            two(li("CJ", 40, 60), jw, pvw, ALU.subtract)
+            pick("v", A("nxf", 0, C), io, A("lnx", 0, 20))
         scalar1(li("W", 0, 40), raw(0, 2, True), -2.0, ALU.mult, lf("C0", 0, 1), ALU.add)
-        if t == 0:
-            scalar1(pv16, A("pvr", 15, C, 16), offp, ALU.subtract)
-            scalar1(pvw, A("pvr", 15, C, 16), offp, ALU.subtract)
-
-        def arrived(h):
+        for h in range(2):
             a, z = CUT[h], CUT[h + 1]
             for b in range(4):
                 mm(4 + b, E(b), *codes(n("l_"), a, z), z - a)
                 act(A("ta", AW * b + a, AW * b + z), A("ps%d" % (4 + b), 0, z - a))
-
-        def before():
-            pick("s", EP, NN, pv16)
-
-        for step in ((lambda: arrived(0), before) if t == 0 else (before, lambda: arrived(0))):
-            step()
-        arrived(1)
-        if t == 0:
-            two(li("CJ", 0, 20), pvw, nxw, ALU.subtract)
-            two(li("CJ", 20, 40), jw, nxw, ALU.subtract)
-            two(li("CJ", 40, 60), jw, pvw, ALU.subtract)
         diagonal(raw(2), EP, C)
         scalar1(li("W", 40, 60), raw(2, 1, True), -2.0, ALU.mult, lf("C0", 1, 2), ALU.add)
         scalar1(li("P", 0, 60), li("W", 0, 60), 1, ALU.arith_shift_right, 1, ALU.bitwise_and)
         two(lf("Q", 40, 120, 2), li("P", 20, 60), li("W", 20, 60), ALU.mult)
         two(lf("Q", 1, 120, 2), li("P", 0, 60), li("CJ", 0, 60), ALU.mult)
-        two(lf("S1", 0, 80), lf("Q", 0, 80), lf("Q", 80, 160), ALU.add)
-        two(lf("ZY", 0, 40), lf("S1", 0, 40), lf("S1", 40, 80), ALU.add)
 
         def parts(q, b, i, off):
             pick(q, A(n("at"), 4 * i + b, 4 * P2, 8), A("ta", AW * b, AW * b + C + 1), off)
@@ -403,9 +394,11 @@ def rank_program(g, core, T, topo):
         diagonal(lh("NXR", 0, K), lh("NXA", 0, K), K)
         parts("v", 1, 0, ll)
         scalar1(sn, lh("NXR", 15, K, 16), offp, ALU.subtract)
-        scalar1(lf("TH", 0, 1), A(n("ll"), 5, 6), C + 2.0, ALU.add)
+        two(lf("S1", 0, 80), lf("Q", 0, 80), lf("Q", 80, 160), ALU.add)
         for b in range(4):
             parts("vvss"[b], b, 1, sn)
+        two(lf("ZY", 0, 40), lf("S1", 0, 40), lf("S1", 40, 80), ALU.add)
+        scalar1(lf("TH", 0, 1), A(n("ll"), 5, 6), C + 2.0, ALU.add)
         quant(*codes(n("a_"), 0, P2), A(n("at"), 0, 4 * P2))
         for b in range(4):
             mm(4 + b, W(b), *codes(n("a_"), 0, P2), P2)
@@ -438,7 +431,7 @@ def rank_program(g, core, T, topo):
         for a, z in runs:
             scalar1(lu("H4", a // 4, z // 4), lh("VR", a + 3, z, 4), 4.0, ALU.mult, lf("C4", 0, 1), ALU.add)
         for h in range(2):
-            for q, a, z in DEAL[2 * h:2 * h + 2]:
+            for q, a, z in DEAL[h]:
                 pick(q, A("x%d" % (t + 1), 4 * a, 4 * z), tp, lu("H4", a // 4, z // 4))
             state_codes(t + 1, h)
             if h == 0 and t + 1 < R:

@@ -5,14 +5,26 @@ ALU = AluOpType
 ACT = ActivationFunctionType
 C, K, R, N = 320, 80, 3, 4
 CUT = (0, 192, C)
-DEAL = ((("s", 0, 96), ("v", 96, 192), ("v", 192, 216)), (("s", 216, 296), ("v", 296, C)))
+DEAL = ((("s", 0, 96), ("v", 96, 192), ("v", 192, 224)), (("s", 224, 312), ("v", 312, C)))
+PIECES = ((0, "c", 0, CUT[1]), (1, "s", 0, C), (1, "c", CUT[1], C))
+BANK = ((4, 5, 6, 7), (0, 4, 5, 6))
+START = "offp c0 e0 nx16 e1 prev qu q0 up p0 e2 q1 p1 dpv"
+ROUND = """
+    T0 T1  F0 G0 F1 G1 *pv16 *pvw M0 M1 FN own0 dF T2 E B *e3 T3  count clamp N sum n dN xv xs list
+    u00 u01 u02 u03 u10 *pad *wd *nxl *nxw  EP *nxf v00 v01 s02 s03 u11 u12 u13 dE *cj w s10 v11 s12 s13 bit
+    nx *v fs2 fs3 fs0 fv1 dnx PR TH sn qa0 W0 X sv0 sv1 ss2 ss3 S1 qa1  Hs00 Hs01 Hs02 Hv03 W1 ZY qh0 P0
+    U Hs10 Hv11 Hs12 Hv13 PS RR qh1 P1 IDX *c4 HB own1 own2 own3 qv
+"""
 P2 = 2 * K
 TW = C + P2
 AW = C + 16
 OFF, BIG = 1024.0, 4096.0
 HALF = "float16"
-SKIP = 16
+NS, NV = 3, 2
+SKIP = 8 * NS
 NP = C // 2 - SKIP
+N0 = 64.0
+FWD = C / 2 + N0 - 1
 
 
 def _layout(sizes, align):
@@ -23,25 +35,25 @@ def _layout(sizes, align):
     return at, pos
 
 
-LB, LBW = _layout([("Z", NP), ("M", C), ("PAD", 16), ("B", C), ("F", C), ("G", C), ("FN", C), ("E", C + 2), ("NN", C), ("EP", C),
-                   ("JS", C), ("JV", 3 * NP), ("WD", 2 * C), ("MW", 32), ("M0", 32), ("M1", 32), ("D16", C), ("D4", C)], 16)
-LH, LHW = _layout([("NXA", K), ("NXR", K), ("RAW", 3 * C), ("SC", 3 * NP), ("V", C), ("VR", C)], 16)
-LF, LFW = _layout([("HB", C), ("ACC", 2), ("PS", K), ("Q", 160), ("S1", 80), ("ZY", 40), ("DU", 40), ("RR", 40), ("TH", 1), ("JW", 20),
-                   ("PVW", 20), ("KB", 2), ("LO", 3), ("HI", 3), ("INIT", 3), ("OFFP", 2), ("C0", 2), ("O4", 1), ("C4", 1)], 8)
-LI, LIW = _layout([("J0", 20), ("MV", 64), ("PI", 20), ("PJ", 20), ("PT", 1), ("MD", 32), ("W", 60), ("P", 60), ("CJ", 60)], 8)
-LU, LUW = _layout([("UL", 8), ("PJ", 20), ("PV", 20), ("SN", 6), ("IDX", 20), ("H4", 80)], 8)
+LB, LBW = _layout([("Z", 144), ("M", C), ("PAD", 16), ("B", C), ("F", C), ("G", C), ("FN", C), ("E", C + 2), ("NN", C), ("EP", C),
+                   ("JS", NS * P2), ("JV", NV * NP), ("WD", 2 * C), ("MW", 32), ("M0", 32), ("M1", 32), ("D16", C), ("D4", C)], 16)
+LH, LHW = _layout([("NXA", K), ("NXR", K), ("RAW", 3 * C), ("SC", NV * NP), ("V", C), ("VR", C)], 16)
+LF, LFW = _layout([("HB", C), ("ACC", NS), ("PS", K), ("Q", 160), ("S1", 80), ("ZY", 40), ("DU", 40), ("RR", 40), ("TH", 1), ("JW", 20),
+                   ("PVW", 20), ("KB", NS), ("LO", NV), ("HI", NV), ("INIT", NV), ("OFFP", 1), ("C0", 1), ("O4", 1), ("C4", 1)], 8)
+LI, LIW = _layout([("MV", 64), ("PI", 20), ("PJ", 20), ("PT", 1), ("MD", 32), ("W", 60), ("P", 60), ("CJ", 60)], 8)
+LU, LUW = _layout([("UL", 8), ("PJ", 20), ("PV", 20), ("SN", 6), ("IDX", 20), ("H4", 80), ("NXL", 20)], 8)
 
 X4 = "float8_e4m3fn_x4"
 SCRATCH = {
-    "iotaf": ("sbuf", [128, 2 * C], "float32"), "ones": ("sbuf", [128, 128], "bfloat16"), "eb": ("sbuf", [128, 516], "bfloat16"),
+    "iotaf": ("sbuf", [128, 2 * C], "float32"), "ones": ("sbuf", [128, 144], "bfloat16"), "eb": ("sbuf", [128, 516], "bfloat16"),
     "ec": ("sbuf", [128, 512], X4), "es": ("sbuf", [128, 512], "uint8"),
     "ut": ("sbuf", [128, 512], "bfloat16"), "uc": ("sbuf", [128, 128], X4), "us": ("sbuf", [128, 128], "uint8"),
     "upc": ("sbuf", [128, 128], X4), "ups": ("sbuf", [128, 128], "uint8"),
     "vt": ("sbuf", [128, 512], "bfloat16"), "vc": ("sbuf", [128, 128], X4), "vs": ("sbuf", [128, 128], "uint8"),
     "lwc": ("sbuf", [128, 512], X4), "lws": ("sbuf", [128, 512], "uint8"),
-    "nxi": ("sbuf", [128, 20], "int32"), "nx16": ("sbuf", [128, 20], "uint16"), "lnx": ("sbuf", [128, 20], "uint16"),
+    "nxi": ("sbuf", [128, 20], "int32"), "nx16": ("sbuf", [128, 20], "uint16"), "lnx": ("sbuf", [128, 20], "int32"),
     "nxf": ("sbuf", [128, AW], "float32"), "pvf": ("sbuf", [128, C], "float32"), "pvr": ("sbuf", [128, C], HALF),
-    "ta": ("sbuf", [128, 4 * AW], "bfloat16"),
+    "ta": ("sbuf", [128, 4 * AW], "bfloat16"), "tp": ("sbuf", [128, 4 * TW], "bfloat16"),
     "lb": ("sbuf", [128, LBW], "bfloat16"), "lf": ("sbuf", [128, LFW], "float32"), "lh": ("sbuf", [128, LHW], HALF),
     "li": ("sbuf", [128, LIW], "int32"), "lu": ("sbuf", [128, LUW], "uint16"),
     "yt": ("sbuf", [128, C], "float32"), "ott": ("sbuf", [128, C], "float32"),
@@ -51,21 +63,21 @@ for _t in range(R + 1):
     SCRATCH["qc%d" % _t] = ("sbuf", [128, C], X4)
     SCRATCH["qs%d" % _t] = ("sbuf", [128, C], "uint8")
 for _t in range(R):
-    SCRATCH["tp%d" % _t] = ("sbuf", [128, 4 * TW], "bfloat16")
     SCRATCH["lc%d" % _t] = ("sbuf", [128, C], X4)
     SCRATCH["ls%d" % _t] = ("sbuf", [128, C], "uint8")
-    SCRATCH["at%d" % _t] = ("sbuf", [128, 4 * P2], "bfloat16")
-    SCRATCH["ac%d" % _t] = ("sbuf", [128, P2], X4)
-    SCRATCH["as%d" % _t] = ("sbuf", [128, P2], "uint8")
-    SCRATCH["hc%d" % _t] = ("sbuf", [128, P2], X4)
-    SCRATCH["hs%d" % _t] = ("sbuf", [128, P2], "uint8")
     SCRATCH["sl%d" % _t] = ("sbuf", [128, 6], "uint16")
     SCRATCH["ll%d" % _t] = ("sbuf", [128, 6], "uint16")
+for _i in range(2):
+    SCRATCH["at%d" % _i] = ("sbuf", [128, 512], "bfloat16")
+    SCRATCH["ac%d" % _i] = ("sbuf", [128, 128], X4)
+    SCRATCH["as%d" % _i] = ("sbuf", [128, 128], "uint8")
+    SCRATCH["hc%d" % _i] = ("sbuf", [128, P2], X4)
+    SCRATCH["hs%d" % _i] = ("sbuf", [128, P2], "uint8")
 for _b in range(8):
     SCRATCH["ps%d" % _b] = ("psum", [128, 512], "float32")
 
-SEMAPHORES = (["cv", "cs", "ct", "cg", "loc", "rn"] + ["d%d" % i for i in range(20)]
-              + [s + "%d" % t for t in range(R) for s in ("ra", "rb", "rs", "rl")])
+SEMAPHORES = (["cv", "cs", "ct", "cg", "loc", "rn"] + ["d%d" % i for i in range(20)] + ["rl%d" % t for t in range(R)]
+              + ["a%d_%d" % (t, i) for t in range(R) for i in range(6)])
 
 
 def _cols(a, b, step=1):
@@ -93,8 +105,6 @@ def _machine(g, T):
         for acc, wr in [(a, True) for a in writes] + [(a, False) for a in reads]:
             for mask, oq, sem, val, owr in hist.get(acc[1], []):
                 if not mask & acc[2]:
-                    continue
-                if wr and not owr and oq == q:
                     continue
                 if not wr and not owr and (oq == q or not acc[1].startswith("ps")):
                     continue
@@ -127,9 +137,9 @@ def _machine(g, T):
         clock[(sem, 16)] = dict(known[q])
         note("d", sem, 16, writes, reads)
 
-    def send(out, in_, rsem, where, reads, engines):
+    def send(out, in_, rsem, where, reads):
         order("g", [], reads)
-        total["loc"] = total.get("loc", 0) + engines
+        total["loc"] = total.get("loc", 0) + where[3]
         g.remote_dma(out, in_, T.sem[rsem], T.sem.loc, where[0], where[1], where[2])
 
     def lands(writes, rsem, engines):
@@ -150,8 +160,7 @@ def rank_program(g, core, T, topo):
     op, dma, send, lands, close = _machine(g, T)
     dst, src = T.cores[(rank + 1) % N], T.cores[rank - 1]
     rid, pid = topo.addr(dst)[:2]
-    where = (pid, rid, topo.mask(core, dst))
-    n_out, n_in = len(topo.engines(core, dst)), len(topo.engines(src, core))
+    where = (pid, rid, topo.mask(core, dst), len(topo.engines(core, dst)))
 
     def A(name, a, b, step=1):
         return (T[name][:, a:b:step] if step > 1 else T[name][:, a:b], name, 1 if name.startswith("ps") else _cols(a, b, step))
@@ -164,11 +173,11 @@ def rank_program(g, core, T, topo):
     def U8(acc):
         return acc[0].bitcast(dt.uint8)
 
-    def E(b):
-        return A("ec", 128 * b, 128 * b + 128), A("es", 128 * b, 128 * b + 128)
+    def codes(name, a, b):
+        return A(name.replace("_", "c"), a, b), A(name.replace("_", "s"), a, b)
 
-    def W(b):
-        return A("lwc", 128 * b, 128 * b + 128), A("lws", 128 * b, 128 * b + 128)
+    def E(b):
+        return codes("e_", 128 * b, 128 * b + 128)
 
     def fill(out, value):
         op("v", lambda q: q.memset(out[0], value), [out], [])
@@ -204,12 +213,12 @@ def rank_program(g, core, T, topo):
     def diagonal(raw, rows, n, mask="D16"):
         scan(raw, lb(mask, 0, n), rows, ALU.add, ALU.max)
 
-    def quant(c, s, tile):
-        op("v", lambda q: q.quantize_mx(c[0], s[0], tile[0]), [c, s], [tile])
+    def quant(cs, tile):
+        op("v", lambda q: q.quantize_mx(cs[0][0], cs[1][0], tile[0]), list(cs), [tile])
 
-    def mm(bank, w, xc, xs, n):
+    def mm(bank, w, x, n):
         out = A("ps%d" % bank, 0, n)
-        op("t", lambda q: q.matmul_mx(out[0], w[0][0], w[1][0], xc[0], xs[0], True, True), [out], [w[0], w[1], xc, xs])
+        op("t", lambda q: q.matmul_mx(out[0], w[0][0], w[1][0], x[0][0], x[1][0], True, True), [out], list(w + x))
 
     def act(out, in_, scale=None, bias=None):
         if bias is not None:
@@ -232,198 +241,197 @@ def rank_program(g, core, T, topo):
     def iota_f(out, pattern, base):
         op("g", lambda q: q.iota(out[0], pattern, base, 0, allow_small_or_imprecise_dtypes=True), [out], [])
 
-    def codes(name, a, b):
-        return A(name.replace("_", "c"), a, b), A(name.replace("_", "s"), a, b)
+    up = codes("up_", 0, 128)
 
-    def state_codes(t, h):
-        a, b = CUT[h], CUT[h + 1]
-        quant(A("qc%d" % t, a, b), A("qs%d" % t, a, b), A("x%d" % t, 4 * a, 4 * b))
+    def state(t, h):
+        a, z = CUT[h], CUT[h + 1]
+        quant(codes("q_%d" % t, a, z), A("x%d" % t, 4 * a, 4 * z))
+        for i, (run, kind, c0, c1) in enumerate(PIECES if t < R else ()):
+            if run == h:
+                out, in_ = A("l%s%d" % (kind, t), c0, c1), A("q%s%d" % (kind, t), c0, c1)
+                send(U8(out) if kind == "c" else out[0], U8(in_) if kind == "c" else in_[0], "a%d_%d" % (t, i), where, [in_])
 
-    def send_codes(t, h):
-        i = A("qc%d" % t, CUT[h], CUT[h + 1])
-        send(U8(A("lc%d" % t, CUT[h], CUT[h + 1])), U8(i), ("ra%d", "rb%d")[h] % t, where, [i], n_out)
+    def scores(t, h):
+        a, z = CUT[h], CUT[h + 1]
+        mm(4 + h, up if t < R else codes("v_", 0, 128), codes("q_%d" % t, a, z), z - a)
 
-    def send_scales(t):
-        i = A("qs%d" % t, 0, C)
-        send(A("ls%d" % t, 0, C)[0], i[0], "rs%d" % t, where, [i], n_out)
-
-    load("y", "nxi", 0, 20, T.nx[:, :])
-    load("s", "ut", 0, 512, T.u[:, :])
+    load("s", "nxi", 0, 20, T.nx[:, :])
+    load("y", "ut", 0, 512, T.u[:, :])
     load("y", "x0", 0, 4 * CUT[1], T.x[:, 0:4 * CUT[1]])
     load("y", "x0", 4 * CUT[1], 4 * C, T.x[:, 4 * CUT[1]:4 * C])
     w = A("lwc", 0, 512)
     dma("y", U8(w), T.wc[:, :], [w], [])
     load("y", "lws", 0, 512, T.ws[:, :])
+    n_in = len(topo.engines(src, core))
     lands([A("lnx", 0, 20)], "rn", n_in)
     for t in range(R):
-        lands([A("lc%d" % t, 0, CUT[1])], "ra%d" % t, n_in)
-        lands([A("lc%d" % t, CUT[1], C)], "rb%d" % t, n_in)
-        lands([A("ls%d" % t, 0, C)], "rs%d" % t, n_in)
+        for i, (run, kind, a, b) in enumerate(PIECES):
+            lands([A("l%s%d" % (kind, t), a, b)], "a%d_%d" % (t, i), n_in)
         lands([A("ll%d" % t, 0, 6)], "rl%d" % t, n_in)
 
     nx16, pv16, nxw, jw, pvw = A("nx16", 0, 20), lu("PV", 0, 20), lf("Q", 121, 160, 2), lf("JW", 0, 20), lf("PVW", 0, 20)
-    offp, io = lf("OFFP", 0, 1), A("iotaf", 0, C)
-    fill(A("ones", 0, 128), 1.0)
+    offp, io, ones, pf, ul = lf("OFFP", 0, 1), A("iotaf", 0, C), A("ones", 0, 144), A("pvf", 0, C), lu("UL", 0, 8)
+    fill(ones, 1.0)
     fill(A("eb", 0, 516), 0.0)
-    iota(li("J0", 0, 20), [[16, 20]], 0, 0)
     iota(li("MV", 0, 64), [[1, 64]], 128, -1)
     iota(li("PI", 0, 20), [[0, 20]], 0, 1)
-    iota_f(io, [[1, C]], 0)
+    iota_f(A("iotaf", 0, P2), [[1, P2]], 0)
     e, o = A("eb", 3, 515, 4), A("ones", 0, 128)
     op("g", lambda q: q.affine_select(e[0], o[0], [[-1, 128]], ALU.is_equal, 0.0, 0, 1), [e], [o])
-    const(lb("Z", 0, 128), 128, 0.0)
-    const(lb("Z", 128, NP), NP - 128, 0.0)
+    send(A("lnx", 0, 20)[0], A("nxi", 0, 20)[0], "rn", where, [A("nxi", 0, 20)])
+    const(lb("Z", 0, 144), 144, 0.0)
     const(lb("PAD", 0, 16), 16, 0.0)
-    const(lf("Q", 0, 160, 2), 80, 0.0)
+    const(lf("Q", 120, 160, 2), 20, -3.0)
     const(lf("DU", 0, 40, 2), 20, -BIG)
+    act(A("iotaf", P2, C), A("iotaf", 0, P2), 1.0, float(P2))
     const(A("ta", C, 4 * AW, AW), 4, 0.0)
     const(A("nxf", C, C + 1), 1, float(C))
-    copy(lu("UL", 0, 8), li("J0", 0, 8))
     scalar1(li("MD", 0, 16), li("MV", 0, 16), 15, ALU.bitwise_and)
     scalar1(li("MD", 16, 32), li("MV", 3, 64, 4), 2, ALU.arith_shift_right, 3, ALU.bitwise_and)
     scalar1(li("PJ", 0, 20), li("PI", 0, 20), 15, ALU.bitwise_and)
     scalar1(lb("M0", 0, 32), li("MD", 0, 32), 0.0, ALU.is_equal, -BIG, ALU.mult)
     scalar1(lb("M1", 0, 32), li("MD", 0, 32), 1.0, ALU.is_equal, OFF, ALU.mult)
     copy(lu("PJ", 0, 20), li("PJ", 0, 20))
-    two(jw, li("J0", 0, 20), li("PJ", 0, 20), ALU.add)
     two(lb("MW", 0, 32), lb("M0", 0, 32), lb("M1", 0, 32), ALU.add)
-    scalar1(li("PT", 0, 1), li("PI", 0, 1), 3, ALU.bitwise_and)
-    scalar1(lf("OFFP", 0, 2), lb("MW", 15, 32, 16), -1.0, ALU.is_gt, OFF, ALU.mult)
-    scalar1(lf("O4", 0, 1), lb("MW", 31, 32), -1.0, ALU.is_gt, -4 * OFF, ALU.mult)
-    act(lf("KB", 0, 2), lf("JW", 0, 2), 2.0, 1.0)
-    act(lf("LO", 0, 3), lf("JW", 2, 5), 2.0)
-    act(lf("HI", 0, 3), lf("JW", 2, 5), 2.0, 2.0)
-    act(lf("INIT", 0, 3), lf("JW", 2, 5), 2.0 * NP, float(C))
+    copy(ul, A("iotaf", 0, 128, 16))
+    two(jw, A("iotaf", 0, C, 16), li("PJ", 0, 20), ALU.add)
+    act(lf("KB", 0, NS), lf("JW", 0, NS), 2.0, 1.0)
+    act(lf("LO", 0, NV), lf("JW", NS, 5), 2.0)
+    act(lf("HI", 0, NV), lf("JW", NS, 5), 2.0, 2.0)
+    act(lf("INIT", 0, NV), lf("JW", NS, 5), 2.0 * NP, float(C))
     pick("s", lb("D16", 0, C), lb("MW", 0, 16), lu("PJ", 0, 20))
-    copy(nx16, A("nxi", 0, 20))
-    send(A("lnx", 0, 20)[0], nx16[0], "rn", where, [nx16], n_out)
-    copy(nxw, A("nxi", 0, 20))
-    two(lf("C4", 0, 1), lf("O4", 0, 1), li("PT", 0, 1), ALU.add)
-    for i in range(2):
-        act(lf("C0", i, i + 1), offp, 2.0, 2.0 * C + i)
-    pf = A("pvf", 0, C)
-    op("v", lambda q: q.tensor_copy(pf[0].indirect(nx16[0]), io[0]), [pf], [io, nx16])
-    quant(A("uc", 0, 128), A("us", 0, 128), A("ut", 0, 512))
-    diagonal(A("pvr", 0, C), pf, C)
-    up, ic_, ul = (A("upc", 0, 128), A("ups", 0, 128)), A("uc", 0, 128), lu("UL", 0, 8)
-    op("v", lambda q: q.tensor_copy(up[0][0].bitcast(dt.uint32), ic_[0].bitcast(dt.uint32).indirect(ul[0])), [up[0]], [ic_, ul])
-    pick("s", up[1], A("us", 0, 128), ul)
-    pick("s", lb("D4", 0, C), lb("MW", 16, 32), lu("PJ", 0, 20))
-    scalar1(pv16, A("pvr", 15, C, 16), offp, ALU.subtract)
-    scalar1(pvw, A("pvr", 15, C, 16), offp, ALU.subtract)
-    state_codes(0, 0)
-    send_codes(0, 0)
-    mm(4, up, *codes("q_0", 0, CUT[1]), CUT[1])
-    for b in range(4):
-        quant(E(b)[0], E(b)[1], A("eb", 3 - b, 515 - b))
-        if b == 1:
-            state_codes(0, 1)
 
     F, G, FN, NN, EP = lb("F", 0, C), lb("G", 0, C), lb("FN", 0, C), lb("NN", 0, C), lb("EP", 0, C)
 
     def raw(i, k=1, last=False):
         return lh("RAW", C * i + 15, C * (i + k), 16) if last else lh("RAW", C * i, C * (i + k))
 
-    for t in range(R):
+    def u_on_groups():
+        uc = A("uc", 0, 128)
+        op("v", lambda q: q.tensor_copy(up[0][0].bitcast(dt.uint32), uc[0].bitcast(dt.uint32).indirect(ul[0])), [up[0]], [uc, ul])
+        pick("s", up[1], A("us", 0, 128), ul)
+        pick("s", lb("D4", 0, C), lb("MW", 16, 32), lu("PJ", 0, 20))
+
+    def steps(t):
         n = lambda s: "%s%d" % (s, t)
-        tp = A(n("tp"), 0, 4 * TW)
-        send_scales(t)
-        send_codes(t, 1)
-        mm(5, up, *codes(n("q_"), CUT[1], C), C - CUT[1])
-        for b in range(4):
-            mm(b, E(b), *codes(n("q_"), 0, C), C)
-        for h in range(2):
-            a, z = CUT[h], CUT[h + 1]
-            scalar1(lb("F", a, z), A("ps%d" % (4 + h), 0, z - a), 0.0, ALU.is_gt)
-            scalar1(lb("G", a, z), A("ps%d" % (4 + h), 0, z - a), 0.0, ALU.is_gt, 1.0, ALU.subtract)
-        for h in range(2):
-            a, z = CUT[h], CUT[h + 1]
-            two_at(lb("M", a, z), F, A("nx16", a // 16, z // 16), lb("G", a, z), ALU.is_le)
-        pick("s", FN, F, nx16)
-        diagonal(raw(0), F, C)
-        scan(lb("E", 0, C + 2), lb("M", 0, C + 2), lb("M", -1, C + 1), ALU.add, ALU.add)
-        scan(lb("B", 0, C), FN, G, ALU.max, ALU.mult)
-        sl = A(n("sl"), 0, 6)
-        for m in range(2):
-            j, acc, kb, pairs = lb("JS", P2 * m, P2 * m + P2), lf("ACC", m, m + 1), lf("KB", m, m + 1), lb("E", 1, C, 2)
-            op("s", lambda q, j=j, acc=acc, kb=kb: q.activation(j[0], pairs[0], ACT.Sign, bias=kb[0], scale=-1.0, accum_out=acc[0]),
-               [j, acc], [pairs, kb])
-        for m in range(3):
-            scalar1(lb("JV", NP * m, NP * m + NP), lb("E", 2 * SKIP + 1, C, 2), lf("LO", m, m + 1), ALU.max, lf("HI", m, m + 1), ALU.min)
-        for m in range(3):
-            scan(lh("SC", NP * m, NP * m + NP), lb("Z", 0, NP), lb("JV", NP * m, NP * m + NP), ALU.add, ALU.subtract, lf("INIT", m, m + 1))
-        scalar1(A(n("sl"), 5, 6), lb("E", C, C + 1), float(P2), ALU.min, 2.0, ALU.mult)
-        scan(NN, lb("B", 0, C), lb("B", -1, C - 1), ALU.add, ALU.add, C / 2.0)
-        copy(A(n("sl"), 2, 5), lh("SC", NP - 1, 3 * NP, NP))
-        scalar1(A(n("sl"), 0, 2), lf("ACC", 0, 2), C / 2.0, ALU.add)
-        send(A(n("ll"), 0, 6)[0], sl[0], n("rl"), where, [sl], n_out)
-        pick("s", EP, NN, pv16)
-        diagonal(raw(1), NN, C)
-        if t == 0:
-            iota_f(A("iotaf", C, 2 * C), [[2, K], [0, 4]], C)
-            iota_f(lb("WD", 0, 2 * C), [[0, 2 * C]], 0)
-            two(li("CJ", 0, 20), pvw, nxw, ALU.subtract)
-            two(li("CJ", 20, 40), jw, nxw, ALU.subtract)
-            two(li("CJ", 40, 60), jw, pvw, ALU.subtract)
-            pick("v", A("nxf", 0, C), io, A("lnx", 0, 20))
-        scalar1(li("W", 0, 40), raw(0, 2, True), -2.0, ALU.mult, lf("C0", 0, 1), ALU.add)
-        for h in range(2):
-            a, z = CUT[h], CUT[h + 1]
-            for b in range(4):
-                mm(4 + b, E(b), *codes(n("l_"), a, z), z - a)
-                act(A("ta", AW * b + a, AW * b + z), A("ps%d" % (4 + b), 0, z - a))
-        diagonal(raw(2), EP, C)
-        scalar1(li("W", 40, 60), raw(2, 1, True), -2.0, ALU.mult, lf("C0", 1, 2), ALU.add)
-        scalar1(li("P", 0, 60), li("W", 0, 60), 1, ALU.arith_shift_right, 1, ALU.bitwise_and)
-        two(lf("Q", 40, 120, 2), li("P", 20, 60), li("W", 20, 60), ALU.mult)
-        two(lf("Q", 1, 120, 2), li("P", 0, 60), li("CJ", 0, 60), ALU.mult)
+        ll, sn, pairs = A(n("ll"), 0, 5), lu("SN", 0, 5), lb("E", 1, C, 2)
 
-        def parts(q, b, i, off):
-            pick(q, A(n("at"), 4 * i + b, 4 * P2, 8), A("ta", AW * b, AW * b + C + 1), off)
+        def count(m):
+            j, acc, kb = lb("JS", P2 * m, P2 * m + P2), lf("ACC", m, m + 1), lf("KB", m, m + 1)
+            op("s", lambda q: q.activation(j[0], pairs[0], ACT.Sign, bias=kb[0], scale=-1.0, accum_out=acc[0]), [j, acc], [pairs, kb])
 
-        def own(b):
-            act(A(n("tp"), b, 4 * C, 4), A("ps%d" % b, 0, C))
+        def each(k, f):
+            return lambda: [f(i) for i in range(k)]
 
-        ll, sn = A(n("ll"), 0, 5), lu("SN", 0, 5)
-        pick("v", lh("NXA", 0, K), A("nxf", 0, C + 1), ll)
-        if t == 0:
-            load("y", "vt", 0, 512, T.v[:, :], [ll])
-        parts("s", 2, 0, ll)
-        parts("s", 3, 0, ll)
-        parts("v", 0, 0, ll)
-        diagonal(lh("NXR", 0, K), lh("NXA", 0, K), K)
-        parts("v", 1, 0, ll)
-        scalar1(sn, lh("NXR", 15, K, 16), offp, ALU.subtract)
-        two(lf("S1", 0, 80), lf("Q", 0, 80), lf("Q", 80, 160), ALU.add)
+        s = {
+            "prev": lambda: op("v", lambda q: q.tensor_copy(pf[0].indirect(nx16[0]), io[0]), [pf], [io, nx16]),
+            "offp": lambda: scalar1(offp, lb("MW", 15, 16), -1.0, ALU.is_gt, OFF, ALU.mult),
+            "c0": lambda: act(lf("C0", 0, 1), offp, 2.0, 2.0 * FWD + 3),
+            "dpv": lambda: diagonal(A("pvr", 0, C), pf, C),
+            "pv16": lambda: scalar1(pv16, A("pvr", 15, C, 16), offp, ALU.subtract),
+            "pvw": lambda: scalar1(pvw, A("pvr", 15, C, 16), offp, ALU.subtract),
+            "nxw": lambda: copy(nxw, A("nxi", 0, 20)),
+            "cj": lambda: [two(li("CJ", 20 * i, 20 * i + 20), a, b, ALU.subtract) for i, (a, b) in enumerate(((pvw, nxw), (jw, nxw), (jw, pvw)))],
+            "c4": lambda: [scalar1(lf("O4", 0, 1), lb("MW", 31, 32), -1.0, ALU.is_gt, -4 * OFF, ALU.mult),
+                           scalar1(li("PT", 0, 1), li("PI", 0, 1), 3, ALU.bitwise_and),
+                           two(lf("C4", 0, 1), lf("O4", 0, 1), li("PT", 0, 1), ALU.add)],
+            "pad": lambda: [iota_f(A(name, a, z), [[0, z - a]], 0) for name, a, z in (("at0", 4 * K, 512), ("at1", 4 * K, 512), ("tp", 4 * C, 4 * TW))],
+            "nx16": lambda: copy(nx16, A("nxi", 0, 20)),
+            "wd": lambda: [iota_f(A("iotaf", C, 2 * C), [[2, K], [0, 4]], C), iota_f(lb("WD", 0, 2 * C), [[0, 2 * C]], 0)],
+            "nxl": lambda: copy(lu("NXL", 0, 20), A("lnx", 0, 20)),
+            "nxf": lambda: pick("s", A("nxf", 0, C), io, lu("NXL", 0, 20)),
+            "qu": lambda: quant(codes("u_", 0, 128), A("ut", 0, 512)),
+            "up": u_on_groups,
+            "v": lambda: load("y", "vt", 0, 512, T.v[:, :], [ll]),
+            "qv": lambda: t + 1 == R and quant(codes("v_", 0, 128), A("vt", 0, 512)),
+            "FN": lambda: op("s", lambda q: q.activation(FN[0], F[0].indirect(nx16[0]), ACT.Sign), [FN], [F, nx16]),
+            "E": lambda: scan(lb("E", 0, C + 2), lb("M", 0, C + 2), lb("M", -1, C + 1), ALU.add, ALU.add),
+            "count": each(NS, count),
+            "clamp": each(NV, lambda m: scalar1(lb("JV", NP * m, NP * m + NP), lb("E", 2 * SKIP + 1, C, 2), lf("LO", m, m + 1), ALU.max,
+                                               lf("HI", m, m + 1), ALU.min)),
+            "sum": each(NV, lambda m: scan(lh("SC", NP * m, NP * m + NP), lb("Z", 0, NP), lb("JV", NP * m, NP * m + NP), ALU.add,
+                                          ALU.subtract, lf("INIT", m, m + 1))),
+            "n": lambda: scalar1(A(n("sl"), 5, 6), lb("E", C, C + 1), float(P2), ALU.min, 2.0, ALU.mult),
+            "xv": lambda: copy(A(n("sl"), NS, 5), lh("SC", NP - 1, NV * NP, NP)),
+            "xs": lambda: scalar1(A(n("sl"), 0, NS), lf("ACC", 0, NS), C / 2.0, ALU.add),
+            "list": lambda: send(A(n("ll"), 0, 6)[0], A(n("sl"), 0, 6)[0], n("rl"), where, [A(n("sl"), 0, 6)]),
+            "B": lambda: scan(lb("B", 0, C), FN, G, ALU.max, ALU.mult),
+            "N": lambda: scan(NN, lb("B", 0, C), lb("B", -1, C - 1), ALU.add, ALU.add, N0),
+            "EP": lambda: pick("s", EP, NN, pv16),
+            "dF": lambda: diagonal(raw(0), F, C),
+            "dN": lambda: diagonal(raw(1), NN, C),
+            "dE": lambda: diagonal(raw(2), EP, C),
+            "w": lambda: scalar1(li("W", 0, 60), raw(0, 3, True), -2.0, ALU.mult, lf("C0", 0, 1), ALU.add),
+            "bit": lambda: scalar1(li("P", 0, 60), li("W", 0, 60), 1, ALU.arith_shift_right, 1, ALU.bitwise_and),
+            "PR": lambda: two(lf("Q", 0, 120, 2), li("P", 0, 60), li("W", 0, 60), ALU.mult),
+            "X": lambda: two(lf("Q", 1, 120, 2), li("P", 0, 60), li("CJ", 0, 60), ALU.mult),
+            "S1": lambda: two(lf("S1", 0, 80), lf("Q", 0, 80), lf("Q", 80, 160), ALU.add),
+            "ZY": lambda: two(lf("ZY", 0, 40), lf("S1", 0, 40), lf("S1", 40, 80), ALU.add),
+            "TH": lambda: scalar1(lf("TH", 0, 1), A(n("ll"), 5, 6), float(C), ALU.add),
+            "U": lambda: scalar1(lf("DU", 1, 40, 2), lf("ZY", 0, 40, 2), lf("TH", 0, 1), ALU.is_ge, -BIG, ALU.mult),
+            "RR": lambda: scan(lf("RR", 0, 40), lf("DU", 0, 40), lf("ZY", 0, 40), ALU.add, ALU.max),
+            "IDX": lambda: copy(lu("IDX", 0, 20), lf("RR", 1, 40, 2)),
+            "HB": lambda: pick("s", lf("HB", 0, C), A("iotaf", 0, 2 * C), lu("IDX", 0, 20)),
+            "nx": lambda: pick("v", lh("NXA", 0, K), A("nxf", 0, C + 1), ll),
+            "dnx": lambda: diagonal(lh("NXR", 0, K), lh("NXA", 0, K), K),
+            "sn": lambda: scalar1(sn, lh("NXR", 15, K, 16), offp, ALU.subtract),
+            "PS": lambda: act(lf("PS", 0, K), A("ps7", 0, P2, 2)),
+        }
+
+        def run(h):
+            a, z = CUT[h], CUT[h + 1]
+            bank = A("ps%d" % (4 + h), 0, z - a)
+            s["q%d" % h] = lambda: state(t, h)
+            s["p%d" % h] = lambda: scores(t, h)
+            s["F%d" % h] = lambda: scalar1(lb("F", a, z), bank, 0.0, ALU.is_gt, FWD, ALU.mult)
+            s["G%d" % h] = lambda: scalar1(lb("G", a, z), bank, 0.0, ALU.is_gt, 1.0, ALU.subtract)
+            s["M%d" % h] = lambda: two_at(lb("M", a, z), F, A("nx16", a // 16, z // 16), lb("G", a, z), ALU.is_le)
+
+        def element(b):
+            s["e%d" % b] = lambda: quant(E(b), A("eb", 3 - b, 515 - b))
+            s["T%d" % b] = lambda: mm(b, E(b), codes(n("q_"), 0, C), C)
+            s["own%d" % b] = lambda: act(A("tp", b, 4 * C, 4), A("ps%d" % b, 0, C))
+
+        def half(i):
+            s["qa%d" % i] = lambda: quant(codes("a_%d" % i, 0, 128), A("at%d" % i, 0, 512))
+            s["W%d" % i] = each(4, lambda b: mm(BANK[i][b], codes("lw_", 128 * b, 128 * b + 128), codes("a_%d" % i, 0, 128), 128))
+            s["qh%d" % i] = lambda: quant(codes("h_%d" % i, 0, P2), A("tp", 4 * C, 4 * TW))
+            s["P%d" % i] = lambda: mm((7, 0)[i], up, codes("h_%d" % i, 0, P2), P2)
+
+        def made(i, b):
+            out, z = A("tp", 4 * C + 4 * i + b, 4 * TW, 8), A("ps%d" % BANK[i][b], 0, K)
+            s["Hv%d%d" % (i, b)] = lambda: scalar1(out, z, 0.03125, ALU.mult)
+            s["Hs%d%d" % (i, b)] = lambda: act(out, z, 0.03125)
+
+        def arrived(h, b):
+            a, z = CUT[h], CUT[h + 1]
+            out, bank = A("ta", AW * b + a, AW * b + z), A("ps%d" % BANK[h][b], 0, z - a)
+            s["u%d%d" % (h, b)] = lambda: mm(BANK[h][b], E(b), codes(n("l_"), a, z), z - a)
+            s["s%d%d" % (h, b)] = lambda: act(out, bank)
+            s["v%d%d" % (h, b)] = lambda: copy(out, bank)
+
+        def parts(i, q, b):
+            s["fs"[i] + q + str(b)] = lambda: pick(q, A("at%d" % i, b, 4 * K, 4), A("ta", AW * b, AW * b + C + 1), (ll, sn)[i])
+
         for b in range(4):
-            parts("vvss"[b], b, 1, sn)
-        two(lf("ZY", 0, 40), lf("S1", 0, 40), lf("S1", 40, 80), ALU.add)
-        scalar1(lf("TH", 0, 1), A(n("ll"), 5, 6), C + 2.0, ALU.add)
-        quant(*codes(n("a_"), 0, P2), A(n("at"), 0, 4 * P2))
-        for b in range(4):
-            mm(4 + b, W(b), *codes(n("a_"), 0, P2), P2)
-        own(0)
-        own(1)
-        scalar1(lf("DU", 1, 40, 2), lf("ZY", 0, 40, 2), lf("TH", 0, 1), ALU.is_ge, -BIG, ALU.mult)
-        scan(lf("RR", 0, 40), lf("DU", 0, 40), lf("ZY", 0, 40), ALU.add, ALU.max)
-        copy(lu("IDX", 0, 20), lf("RR", 1, 40, 2))
-        for b in range(4):
-            out, z = A(n("tp"), 4 * C + b, 4 * TW, 4), A("ps%d" % (4 + b), 0, P2)
-            if b % 2 == 0:
-                act(out, z, 0.03125)
-            else:
-                scalar1(out, z, 0.03125, ALU.mult)
-        quant(*codes(n("h_"), 0, P2), A(n("tp"), 4 * C, 4 * TW))
-        mm(0, up, *codes(n("h_"), 0, P2), P2)
-        pick("s", lf("HB", 0, C), A("iotaf", 0, 2 * C), lu("IDX", 0, 20))
-        own(2)
-        own(3)
-        if t + 1 == R:
-            quant(A("vc", 0, 128), A("vs", 0, 128), A("vt", 0, 512))
-        copy(lf("PS", 0, K), A("ps0", 0, P2, 2))
-        two(lb("WD", C + 2, 2 * C, 4), lf("PS", 0, K), A("ps0", 1, P2, 2), ALU.is_lt)
+            element(b)
+            for h in range(2):
+                run(h)
+                arrived(h, b)
+                half(h)
+                made(h, b)
+                parts(h, "v", b)
+                parts(h, "s", b)
+        return s
+
+    runs = [(CUT[h], CUT[h + 1]) for h in range(2)]
+    for t in range(R):
+        step = steps(t)
+        for name in (START.split() if t == 0 else []) + ROUND.split():
+            if t == 0 or name[0] != "*":
+                step[name.strip("*")]()
+        two(lb("WD", C, 2 * C, 4), lf("PS", 0, K), A("ps0", 1, P2, 2), ALU.is_lt)
         two(lb("WD", C + 3, 2 * C, 4), lf("PS", 0, K), A("ps0", 1, P2, 2), ALU.is_ge)
-        runs = [(CUT[h], CUT[h + 1]) for h in range(2)]
         for a, z in runs:
             two_at(lh("V", a, z), lb("WD", 0, 2 * C), lu("IDX", a // 16, z // 16), lf("HB", a, z), ALU.add)
         for a, z in runs:
@@ -432,23 +440,23 @@ def rank_program(g, core, T, topo):
             scalar1(lu("H4", a // 4, z // 4), lh("VR", a + 3, z, 4), 4.0, ALU.mult, lf("C4", 0, 1), ALU.add)
         for h in range(2):
             for q, a, z in DEAL[h]:
-                pick(q, A("x%d" % (t + 1), 4 * a, 4 * z), tp, lu("H4", a // 4, z // 4))
-            state_codes(t + 1, h)
-            if h == 0 and t + 1 < R:
-                send_codes(t + 1, 0)
-                mm(4, up, *codes("q_%d" % (t + 1), 0, CUT[1]), CUT[1])
-            if h == 0 and t + 1 == R:
-                mm(4, codes("v_", 0, 128), *codes("q_3", 0, CUT[1]), CUT[1])
-                dma("y", T.oc[:, 0:4 * CUT[1]], U8(A("qc3", 0, CUT[1])), [], [A("qc3", 0, CUT[1])])
+                pick(q, A("x%d" % (t + 1), 4 * a, 4 * z), A("tp", 0, 4 * TW), lu("H4", a // 4, z // 4))
+            state(t + 1, h)
+            scores(t + 1, h)
+            if t + 1 == R:
+                a, z = runs[h]
+                dma("y", T.oc[:, 4 * a:4 * z], U8(A("qc3", a, z)), [], [A("qc3", a, z)])
 
-    mm(5, codes("v_", 0, 128), *codes("q_3", CUT[1], C), C - CUT[1])
+    def scales(q, k):
+        dma(q, T.osc[4 * k:4 * k + 4, :], T.qs3[32 * k:32 * k + 4, 0:C], [], [A("qs3", 0, C)])
+
     act(A("yt", 0, CUT[1]), A("ps4", 0, CUT[1]))
     dma("s", T.y[:, 0:CUT[1]], A("yt", 0, CUT[1])[0], [], [A("yt", 0, CUT[1])])
     copy(A("ott", 0, C), lh("V", 0, C))
-    dma("y", T.oc[:, 4 * CUT[1]:4 * C], U8(A("qc3", CUT[1], C)), [], [A("qc3", CUT[1], C)])
-    for k in range(4):
-        dma("y", T.osc[4 * k:4 * k + 4, :], T.qs3[32 * k:32 * k + 4, 0:C], [], [A("qs3", 0, C)])
-    act(A("yt", CUT[1], C), A("ps5", 0, C - CUT[1]))
+    for k in range(3):
+        scales("y", k)
+    copy(A("yt", CUT[1], C), A("ps5", 0, C - CUT[1]))
     dma("s", T.y[:, CUT[1]:C], A("yt", CUT[1], C)[0], [], [A("yt", CUT[1], C)])
+    scales("s", 3)
     dma("y", T.ot[:, :], T.ott[0:128:16, 0:C], [], [A("ott", 0, C)])
     close()

import numpy as np
from concourse.mybir import dt, AluOpType, AxisListType, ActivationFunctionType

ALU = AluOpType
ACT = ActivationFunctionType
C, K, R, N = 320, 80, 3, 4
CUT = (0, 192, C)
DEAL = ((("s", 0, 96), ("v", 96, 192), ("v", 192, 224)), (("s", 224, 312), ("v", 312, C)))
PIECES = ((0, "c", 0, CUT[1]), (1, "s", 0, C), (1, "c", CUT[1], C))
BANK = ((4, 5, 6, 7), (0, 4, 5, 6))
START = "offp c0 e0 nx16 e1 prev qu q0 up p0 e2 q1 p1 dpv"
ROUND = """
    T0 T1  F0 G0 F1 G1 *pv16 *pvw M0 M1 FN own0 dF T2 E B *e3 T3  count clamp N sum n dN xv xs list
    u00 u01 u02 u03 u10 *pad *wd *nxl *nxw  EP *nxf v00 v01 s02 s03 u11 u12 u13 dE *cj w s10 v11 s12 s13 bit
    nx *v fs2 fs3 fs0 fv1 dnx PR TH sn qa0 W0 X sv0 sv1 ss2 ss3 S1 qa1  Hs00 Hs01 Hs02 Hv03 W1 ZY qh0 P0
    U Hs10 Hv11 Hs12 Hv13 PS RR qh1 P1 IDX *c4 HB own1 own2 own3 qv
"""
P2 = 2 * K
TW = C + P2
AW = C + 16
OFF, BIG = 1024.0, 4096.0
HALF = "float16"
NS, NV = 3, 2
SKIP = 8 * NS
NP = C // 2 - SKIP
N0 = 64.0
FWD = C / 2 + N0 - 1


def _layout(sizes, align):
    at, pos = {}, 0
    for name, n in sizes:
        at[name] = pos
        pos += -(-n // align) * align
    return at, pos


LB, LBW = _layout([("Z", 144), ("M", C), ("PAD", 16), ("B", C), ("F", C), ("G", C), ("FN", C), ("E", C + 2), ("NN", C), ("EP", C),
                   ("JS", NS * P2), ("JV", NV * NP), ("WD", 2 * C), ("MW", 32), ("M0", 32), ("M1", 32), ("D16", C), ("D4", C)], 16)
LH, LHW = _layout([("NXA", K), ("NXR", K), ("RAW", 3 * C), ("SC", NV * NP), ("V", C), ("VR", C)], 16)
LF, LFW = _layout([("HB", C), ("ACC", NS), ("PS", K), ("Q", 160), ("S1", 80), ("ZY", 40), ("DU", 40), ("RR", 40), ("TH", 1), ("JW", 20),
                   ("PVW", 20), ("KB", NS), ("LO", NV), ("HI", NV), ("INIT", NV), ("OFFP", 1), ("C0", 1), ("O4", 1), ("C4", 1)], 8)
LI, LIW = _layout([("MV", 64), ("PI", 20), ("PJ", 20), ("PT", 1), ("MD", 32), ("W", 60), ("P", 60), ("CJ", 60)], 8)
LU, LUW = _layout([("UL", 8), ("PJ", 20), ("PV", 20), ("SN", 6), ("IDX", 20), ("H4", 80), ("NXL", 20)], 8)

X4 = "float8_e4m3fn_x4"
SCRATCH = {
    "iotaf": ("sbuf", [128, 2 * C], "float32"), "ones": ("sbuf", [128, 144], "bfloat16"), "eb": ("sbuf", [128, 516], "bfloat16"),
    "ec": ("sbuf", [128, 512], X4), "es": ("sbuf", [128, 512], "uint8"),
    "ut": ("sbuf", [128, 512], "bfloat16"), "uc": ("sbuf", [128, 128], X4), "us": ("sbuf", [128, 128], "uint8"),
    "upc": ("sbuf", [128, 128], X4), "ups": ("sbuf", [128, 128], "uint8"),
    "vt": ("sbuf", [128, 512], "bfloat16"), "vc": ("sbuf", [128, 128], X4), "vs": ("sbuf", [128, 128], "uint8"),
    "lwc": ("sbuf", [128, 512], X4), "lws": ("sbuf", [128, 512], "uint8"),
    "nxi": ("sbuf", [128, 20], "int32"), "nx16": ("sbuf", [128, 20], "uint16"), "lnx": ("sbuf", [128, 20], "int32"),
    "nxf": ("sbuf", [128, AW], "float32"), "pvf": ("sbuf", [128, C], "float32"), "pvr": ("sbuf", [128, C], HALF),
    "ta": ("sbuf", [128, 4 * AW], "bfloat16"), "tp": ("sbuf", [128, 4 * TW], "bfloat16"),
    "lb": ("sbuf", [128, LBW], "bfloat16"), "lf": ("sbuf", [128, LFW], "float32"), "lh": ("sbuf", [128, LHW], HALF),
    "li": ("sbuf", [128, LIW], "int32"), "lu": ("sbuf", [128, LUW], "uint16"),
    "yt": ("sbuf", [128, C], "float32"), "ott": ("sbuf", [128, C], "float32"),
}
for _t in range(R + 1):
    SCRATCH["x%d" % _t] = ("sbuf", [128, 4 * C], "bfloat16")
    SCRATCH["qc%d" % _t] = ("sbuf", [128, C], X4)
    SCRATCH["qs%d" % _t] = ("sbuf", [128, C], "uint8")
for _t in range(R):
    SCRATCH["lc%d" % _t] = ("sbuf", [128, C], X4)
    SCRATCH["ls%d" % _t] = ("sbuf", [128, C], "uint8")
    SCRATCH["sl%d" % _t] = ("sbuf", [128, 6], "uint16")
    SCRATCH["ll%d" % _t] = ("sbuf", [128, 6], "uint16")
for _i in range(2):
    SCRATCH["at%d" % _i] = ("sbuf", [128, 512], "bfloat16")
    SCRATCH["ac%d" % _i] = ("sbuf", [128, 128], X4)
    SCRATCH["as%d" % _i] = ("sbuf", [128, 128], "uint8")
    SCRATCH["hc%d" % _i] = ("sbuf", [128, P2], X4)
    SCRATCH["hs%d" % _i] = ("sbuf", [128, P2], "uint8")
for _b in range(8):
    SCRATCH["ps%d" % _b] = ("psum", [128, 512], "float32")

SEMAPHORES = (["cv", "cs", "ct", "cg", "loc", "rn"] + ["d%d" % i for i in range(20)] + ["rl%d" % t for t in range(R)]
              + ["a%d_%d" % (t, i) for t in range(R) for i in range(6)])


def _cols(a, b, step=1):
    m = 0
    for c in range(a, b, step):
        m |= 1 << c
    return m


def _machine(g, T):
    queues = {"v": g.vector, "s": g.scalar, "t": g.tensor, "g": g, "y": g.sync}
    total, clock, hist, fresh = {}, {}, {}, [0]
    known = dict((q, {}) for q in queues)

    def wait(q, sem, val):
        if known[q].get(sem, 0) >= val:
            return
        queues[q].wait_ge(T.sem[sem], val)
        for s, n in clock.get((sem, val), {}).items():
            known[q][s] = max(known[q].get(s, 0), n)
        known[q][sem] = max(known[q].get(sem, 0), val)

    def order(q, writes, reads):
        need = {}
        for acc, wr in [(a, True) for a in writes] + [(a, False) for a in reads]:
            for mask, oq, sem, val, owr in hist.get(acc[1], []):
                if not mask & acc[2]:
                    continue
                if not wr and not owr and (oq == q or not acc[1].startswith("ps")):
                    continue
                need[sem] = max(need.get(sem, 0), val)
        need = [(s, n) for s, n in need.items() if known[q].get(s, 0) < n]
        for s, n in need:
            if not any(clock.get(o, {}).get(s, 0) >= n for o in need if o != (s, n)):
                wait(q, s, n)

    def note(q, sem, val, writes, reads):
        for a in writes:
            hist.setdefault(a[1], []).append((a[2], q, sem, val, True))
        for a in reads:
            hist.setdefault(a[1], []).append((a[2], q, sem, val, False))

    def op(q, call, writes, reads):
        order(q, writes, reads)
        sem = "c" + q
        val = total[sem] = total.get(sem, 0) + 1
        call(queues[q]).then_inc(T.sem[sem], 1)
        clock[(sem, val)] = dict(known[q])
        note(q, sem, val, writes, reads)

    def dma(q, out, in_, writes, reads):
        order(q, writes, reads)
        sem = "d%d" % fresh[0]
        fresh[0] += 1
        total[sem] = 16
        queues[q].dma_start(out, in_).then_inc(T.sem[sem], 16)
        clock[(sem, 16)] = dict(known[q])
        note("d", sem, 16, writes, reads)

    def send(out, in_, rsem, where, reads):
        order("g", [], reads)
        total["loc"] = total.get("loc", 0) + where[3]
        g.remote_dma(out, in_, T.sem[rsem], T.sem.loc, where[0], where[1], where[2])

    def lands(writes, rsem, engines):
        total[rsem] = engines
        note("net", rsem, engines, writes, [])

    def close():
        for sem in sorted(total):
            wait("g", sem, total[sem])

    return op, dma, send, lands, close


def rank_program(g, core, T, topo):
    rank = T.rank_of(core)
    if rank is None:
        return
    op, dma, send, lands, close = _machine(g, T)
    dst, src = T.cores[(rank + 1) % N], T.cores[rank - 1]
    rid, pid = topo.addr(dst)[:2]
    where = (pid, rid, topo.mask(core, dst), len(topo.engines(core, dst)))

    def A(name, a, b, step=1):
        return (T[name][:, a:b:step] if step > 1 else T[name][:, a:b], name, 1 if name.startswith("ps") else _cols(a, b, step))

    def part_of(name, at):
        return lambda key, a, b, step=1: A(name, at[key] + a, at[key] + b, step)

    lb, lh, lf, li, lu = part_of("lb", LB), part_of("lh", LH), part_of("lf", LF), part_of("li", LI), part_of("lu", LU)

    def U8(acc):
        return acc[0].bitcast(dt.uint8)

    def codes(name, a, b):
        return A(name.replace("_", "c"), a, b), A(name.replace("_", "s"), a, b)

    def E(b):
        return codes("e_", 128 * b, 128 * b + 128)

    def fill(out, value):
        op("v", lambda q: q.memset(out[0], value), [out], [])

    def copy(out, in_):
        op("v", lambda q: q.tensor_copy(out[0], in_[0]), [out], [in_])

    def pick(q, out, win, off):
        if q == "v":
            op("v", lambda e: e.tensor_copy(out[0], win[0].indirect(off[0])), [out], [win, off])
        else:
            op("s", lambda e: e.activation(out[0], win[0].indirect(off[0]), ACT.Copy), [out], [win, off])

    def scalar1(out, in0, s1, op0, s2=None, op1=None):
        cols = [s for s in (s1, s2) if isinstance(s, tuple)]
        a1, a2 = [s[0] if isinstance(s, tuple) else s for s in (s1, s2)]
        if op1 is None:
            op("v", lambda q: q.tensor_scalar(out[0], in0[0], a1, None, op0), [out], [in0] + cols)
        else:
            op("v", lambda q: q.tensor_scalar(out[0], in0[0], a1, a2, op0, op1), [out], [in0] + cols)

    def two(out, in0, in1, o):
        op("v", lambda q: q.tensor_tensor(out[0], in0[0], in1[0], o), [out], [in0, in1])

    def two_at(out, win, off, in1, o):
        op("v", lambda q: q.tensor_tensor(out[0], win[0].indirect(off[0]), in1[0], o), [out], [win, off, in1])

    def scan(out, d0, d1, op0, op1, first=0.0):
        col = isinstance(first, tuple)
        op("v", lambda q: q.tensor_tensor_scan(out[0], d0[0], d1[0], first[0] if col else first, op0, op1), [out],
           [d0, d1] + ([first] if col else []))

    def diagonal(raw, rows, n, mask="D16"):
        scan(raw, lb(mask, 0, n), rows, ALU.add, ALU.max)

    def quant(cs, tile):
        op("v", lambda q: q.quantize_mx(cs[0][0], cs[1][0], tile[0]), list(cs), [tile])

    def mm(bank, w, x, n):
        out = A("ps%d" % bank, 0, n)
        op("t", lambda q: q.matmul_mx(out[0], w[0][0], w[1][0], x[0][0], x[1][0], True, True), [out], list(w + x))

    def act(out, in_, scale=None, bias=None):
        if bias is not None:
            op("s", lambda q: q.activation(out[0], in_[0], ACT.Identity, bias=bias, scale=scale), [out], [in_])
        elif scale is not None:
            op("s", lambda q: q.activation(out[0], in_[0], ACT.Copy, scale=scale), [out], [in_])
        else:
            op("s", lambda q: q.activation(out[0], in_[0], ACT.Copy), [out], [in_])

    def const(out, n, value):
        act(out, A("ones", 0, n), value)

    def load(q, name, a, b, ap, after=()):
        w = A(name, a, b)
        dma(q, w[0], ap, [w], list(after))

    def iota(out, pattern, base, ch):
        op("g", lambda q: q.iota(out[0], pattern, base, ch), [out], [])

    def iota_f(out, pattern, base):
        op("g", lambda q: q.iota(out[0], pattern, base, 0, allow_small_or_imprecise_dtypes=True), [out], [])

    up = codes("up_", 0, 128)

    def state(t, h):
        a, z = CUT[h], CUT[h + 1]
        quant(codes("q_%d" % t, a, z), A("x%d" % t, 4 * a, 4 * z))
        for i, (run, kind, c0, c1) in enumerate(PIECES if t < R else ()):
            if run == h:
                out, in_ = A("l%s%d" % (kind, t), c0, c1), A("q%s%d" % (kind, t), c0, c1)
                send(U8(out) if kind == "c" else out[0], U8(in_) if kind == "c" else in_[0], "a%d_%d" % (t, i), where, [in_])

    def scores(t, h):
        a, z = CUT[h], CUT[h + 1]
        mm(4 + h, up if t < R else codes("v_", 0, 128), codes("q_%d" % t, a, z), z - a)

    load("s", "nxi", 0, 20, T.nx[:, :])
    load("y", "ut", 0, 512, T.u[:, :])
    load("y", "x0", 0, 4 * CUT[1], T.x[:, 0:4 * CUT[1]])
    load("y", "x0", 4 * CUT[1], 4 * C, T.x[:, 4 * CUT[1]:4 * C])
    w = A("lwc", 0, 512)
    dma("y", U8(w), T.wc[:, :], [w], [])
    load("y", "lws", 0, 512, T.ws[:, :])
    n_in = len(topo.engines(src, core))
    lands([A("lnx", 0, 20)], "rn", n_in)
    for t in range(R):
        for i, (run, kind, a, b) in enumerate(PIECES):
            lands([A("l%s%d" % (kind, t), a, b)], "a%d_%d" % (t, i), n_in)
        lands([A("ll%d" % t, 0, 6)], "rl%d" % t, n_in)

    nx16, pv16, nxw, jw, pvw = A("nx16", 0, 20), lu("PV", 0, 20), lf("Q", 121, 160, 2), lf("JW", 0, 20), lf("PVW", 0, 20)
    offp, io, ones, pf, ul = lf("OFFP", 0, 1), A("iotaf", 0, C), A("ones", 0, 144), A("pvf", 0, C), lu("UL", 0, 8)
    fill(ones, 1.0)
    fill(A("eb", 0, 516), 0.0)
    iota(li("MV", 0, 64), [[1, 64]], 128, -1)
    iota(li("PI", 0, 20), [[0, 20]], 0, 1)
    iota_f(A("iotaf", 0, P2), [[1, P2]], 0)
    e, o = A("eb", 3, 515, 4), A("ones", 0, 128)
    op("g", lambda q: q.affine_select(e[0], o[0], [[-1, 128]], ALU.is_equal, 0.0, 0, 1), [e], [o])
    send(A("lnx", 0, 20)[0], A("nxi", 0, 20)[0], "rn", where, [A("nxi", 0, 20)])
    const(lb("Z", 0, 144), 144, 0.0)
    const(lb("PAD", 0, 16), 16, 0.0)
    const(lf("Q", 120, 160, 2), 20, -3.0)
    const(lf("DU", 0, 40, 2), 20, -BIG)
    act(A("iotaf", P2, C), A("iotaf", 0, P2), 1.0, float(P2))
    const(A("ta", C, 4 * AW, AW), 4, 0.0)
    const(A("nxf", C, C + 1), 1, float(C))
    scalar1(li("MD", 0, 16), li("MV", 0, 16), 15, ALU.bitwise_and)
    scalar1(li("MD", 16, 32), li("MV", 3, 64, 4), 2, ALU.arith_shift_right, 3, ALU.bitwise_and)
    scalar1(li("PJ", 0, 20), li("PI", 0, 20), 15, ALU.bitwise_and)
    scalar1(lb("M0", 0, 32), li("MD", 0, 32), 0.0, ALU.is_equal, -BIG, ALU.mult)
    scalar1(lb("M1", 0, 32), li("MD", 0, 32), 1.0, ALU.is_equal, OFF, ALU.mult)
    copy(lu("PJ", 0, 20), li("PJ", 0, 20))
    two(lb("MW", 0, 32), lb("M0", 0, 32), lb("M1", 0, 32), ALU.add)
    copy(ul, A("iotaf", 0, 128, 16))
    two(jw, A("iotaf", 0, C, 16), li("PJ", 0, 20), ALU.add)
    act(lf("KB", 0, NS), lf("JW", 0, NS), 2.0, 1.0)
    act(lf("LO", 0, NV), lf("JW", NS, 5), 2.0)
    act(lf("HI", 0, NV), lf("JW", NS, 5), 2.0, 2.0)
    act(lf("INIT", 0, NV), lf("JW", NS, 5), 2.0 * NP, float(C))
    pick("s", lb("D16", 0, C), lb("MW", 0, 16), lu("PJ", 0, 20))

    F, G, FN, NN, EP = lb("F", 0, C), lb("G", 0, C), lb("FN", 0, C), lb("NN", 0, C), lb("EP", 0, C)

    def raw(i, k=1, last=False):
        return lh("RAW", C * i + 15, C * (i + k), 16) if last else lh("RAW", C * i, C * (i + k))

    def u_on_groups():
        uc = A("uc", 0, 128)
        op("v", lambda q: q.tensor_copy(up[0][0].bitcast(dt.uint32), uc[0].bitcast(dt.uint32).indirect(ul[0])), [up[0]], [uc, ul])
        pick("s", up[1], A("us", 0, 128), ul)
        pick("s", lb("D4", 0, C), lb("MW", 16, 32), lu("PJ", 0, 20))

    def steps(t):
        n = lambda s: "%s%d" % (s, t)
        ll, sn, pairs = A(n("ll"), 0, 5), lu("SN", 0, 5), lb("E", 1, C, 2)

        def count(m):
            j, acc, kb = lb("JS", P2 * m, P2 * m + P2), lf("ACC", m, m + 1), lf("KB", m, m + 1)
            op("s", lambda q: q.activation(j[0], pairs[0], ACT.Sign, bias=kb[0], scale=-1.0, accum_out=acc[0]), [j, acc], [pairs, kb])

        def each(k, f):
            return lambda: [f(i) for i in range(k)]

        s = {
            "prev": lambda: op("v", lambda q: q.tensor_copy(pf[0].indirect(nx16[0]), io[0]), [pf], [io, nx16]),
            "offp": lambda: scalar1(offp, lb("MW", 15, 16), -1.0, ALU.is_gt, OFF, ALU.mult),
            "c0": lambda: act(lf("C0", 0, 1), offp, 2.0, 2.0 * FWD + 3),
            "dpv": lambda: diagonal(A("pvr", 0, C), pf, C),
            "pv16": lambda: scalar1(pv16, A("pvr", 15, C, 16), offp, ALU.subtract),
            "pvw": lambda: scalar1(pvw, A("pvr", 15, C, 16), offp, ALU.subtract),
            "nxw": lambda: copy(nxw, A("nxi", 0, 20)),
            "cj": lambda: [two(li("CJ", 20 * i, 20 * i + 20), a, b, ALU.subtract) for i, (a, b) in enumerate(((pvw, nxw), (jw, nxw), (jw, pvw)))],
            "c4": lambda: [scalar1(lf("O4", 0, 1), lb("MW", 31, 32), -1.0, ALU.is_gt, -4 * OFF, ALU.mult),
                           scalar1(li("PT", 0, 1), li("PI", 0, 1), 3, ALU.bitwise_and),
                           two(lf("C4", 0, 1), lf("O4", 0, 1), li("PT", 0, 1), ALU.add)],
            "pad": lambda: [iota_f(A(name, a, z), [[0, z - a]], 0) for name, a, z in (("at0", 4 * K, 512), ("at1", 4 * K, 512), ("tp", 4 * C, 4 * TW))],
            "nx16": lambda: copy(nx16, A("nxi", 0, 20)),
            "wd": lambda: [iota_f(A("iotaf", C, 2 * C), [[2, K], [0, 4]], C), iota_f(lb("WD", 0, 2 * C), [[0, 2 * C]], 0)],
            "nxl": lambda: copy(lu("NXL", 0, 20), A("lnx", 0, 20)),
            "nxf": lambda: pick("s", A("nxf", 0, C), io, lu("NXL", 0, 20)),
            "qu": lambda: quant(codes("u_", 0, 128), A("ut", 0, 512)),
            "up": u_on_groups,
            "v": lambda: load("y", "vt", 0, 512, T.v[:, :], [ll]),
            "qv": lambda: t + 1 == R and quant(codes("v_", 0, 128), A("vt", 0, 512)),
            "FN": lambda: op("s", lambda q: q.activation(FN[0], F[0].indirect(nx16[0]), ACT.Sign), [FN], [F, nx16]),
            "E": lambda: scan(lb("E", 0, C + 2), lb("M", 0, C + 2), lb("M", -1, C + 1), ALU.add, ALU.add),
            "count": each(NS, count),
            "clamp": each(NV, lambda m: scalar1(lb("JV", NP * m, NP * m + NP), lb("E", 2 * SKIP + 1, C, 2), lf("LO", m, m + 1), ALU.max,
                                               lf("HI", m, m + 1), ALU.min)),
            "sum": each(NV, lambda m: scan(lh("SC", NP * m, NP * m + NP), lb("Z", 0, NP), lb("JV", NP * m, NP * m + NP), ALU.add,
                                          ALU.subtract, lf("INIT", m, m + 1))),
            "n": lambda: scalar1(A(n("sl"), 5, 6), lb("E", C, C + 1), float(P2), ALU.min, 2.0, ALU.mult),
            "xv": lambda: copy(A(n("sl"), NS, 5), lh("SC", NP - 1, NV * NP, NP)),
            "xs": lambda: scalar1(A(n("sl"), 0, NS), lf("ACC", 0, NS), C / 2.0, ALU.add),
            "list": lambda: send(A(n("ll"), 0, 6)[0], A(n("sl"), 0, 6)[0], n("rl"), where, [A(n("sl"), 0, 6)]),
            "B": lambda: scan(lb("B", 0, C), FN, G, ALU.max, ALU.mult),
            "N": lambda: scan(NN, lb("B", 0, C), lb("B", -1, C - 1), ALU.add, ALU.add, N0),
            "EP": lambda: pick("s", EP, NN, pv16),
            "dF": lambda: diagonal(raw(0), F, C),
            "dN": lambda: diagonal(raw(1), NN, C),
            "dE": lambda: diagonal(raw(2), EP, C),
            "w": lambda: scalar1(li("W", 0, 60), raw(0, 3, True), -2.0, ALU.mult, lf("C0", 0, 1), ALU.add),
            "bit": lambda: scalar1(li("P", 0, 60), li("W", 0, 60), 1, ALU.arith_shift_right, 1, ALU.bitwise_and),
            "PR": lambda: two(lf("Q", 0, 120, 2), li("P", 0, 60), li("W", 0, 60), ALU.mult),
            "X": lambda: two(lf("Q", 1, 120, 2), li("P", 0, 60), li("CJ", 0, 60), ALU.mult),
            "S1": lambda: two(lf("S1", 0, 80), lf("Q", 0, 80), lf("Q", 80, 160), ALU.add),
            "ZY": lambda: two(lf("ZY", 0, 40), lf("S1", 0, 40), lf("S1", 40, 80), ALU.add),
            "TH": lambda: scalar1(lf("TH", 0, 1), A(n("ll"), 5, 6), float(C), ALU.add),
            "U": lambda: scalar1(lf("DU", 1, 40, 2), lf("ZY", 0, 40, 2), lf("TH", 0, 1), ALU.is_ge, -BIG, ALU.mult),
            "RR": lambda: scan(lf("RR", 0, 40), lf("DU", 0, 40), lf("ZY", 0, 40), ALU.add, ALU.max),
            "IDX": lambda: copy(lu("IDX", 0, 20), lf("RR", 1, 40, 2)),
            "HB": lambda: pick("s", lf("HB", 0, C), A("iotaf", 0, 2 * C), lu("IDX", 0, 20)),
            "nx": lambda: pick("v", lh("NXA", 0, K), A("nxf", 0, C + 1), ll),
            "dnx": lambda: diagonal(lh("NXR", 0, K), lh("NXA", 0, K), K),
            "sn": lambda: scalar1(sn, lh("NXR", 15, K, 16), offp, ALU.subtract),
            "PS": lambda: act(lf("PS", 0, K), A("ps7", 0, P2, 2)),
        }

        def run(h):
            a, z = CUT[h], CUT[h + 1]
            bank = A("ps%d" % (4 + h), 0, z - a)
            s["q%d" % h] = lambda: state(t, h)
            s["p%d" % h] = lambda: scores(t, h)
            s["F%d" % h] = lambda: scalar1(lb("F", a, z), bank, 0.0, ALU.is_gt, FWD, ALU.mult)
            s["G%d" % h] = lambda: scalar1(lb("G", a, z), bank, 0.0, ALU.is_gt, 1.0, ALU.subtract)
            s["M%d" % h] = lambda: two_at(lb("M", a, z), F, A("nx16", a // 16, z // 16), lb("G", a, z), ALU.is_le)

        def element(b):
            s["e%d" % b] = lambda: quant(E(b), A("eb", 3 - b, 515 - b))
            s["T%d" % b] = lambda: mm(b, E(b), codes(n("q_"), 0, C), C)
            s["own%d" % b] = lambda: act(A("tp", b, 4 * C, 4), A("ps%d" % b, 0, C))

        def half(i):
            s["qa%d" % i] = lambda: quant(codes("a_%d" % i, 0, 128), A("at%d" % i, 0, 512))
            s["W%d" % i] = each(4, lambda b: mm(BANK[i][b], codes("lw_", 128 * b, 128 * b + 128), codes("a_%d" % i, 0, 128), 128))
            s["qh%d" % i] = lambda: quant(codes("h_%d" % i, 0, P2), A("tp", 4 * C, 4 * TW))
            s["P%d" % i] = lambda: mm((7, 0)[i], up, codes("h_%d" % i, 0, P2), P2)

        def made(i, b):
            out, z = A("tp", 4 * C + 4 * i + b, 4 * TW, 8), A("ps%d" % BANK[i][b], 0, K)
            s["Hv%d%d" % (i, b)] = lambda: scalar1(out, z, 0.03125, ALU.mult)
            s["Hs%d%d" % (i, b)] = lambda: act(out, z, 0.03125)

        def arrived(h, b):
            a, z = CUT[h], CUT[h + 1]
            out, bank = A("ta", AW * b + a, AW * b + z), A("ps%d" % BANK[h][b], 0, z - a)
            s["u%d%d" % (h, b)] = lambda: mm(BANK[h][b], E(b), codes(n("l_"), a, z), z - a)
            s["s%d%d" % (h, b)] = lambda: act(out, bank)
            s["v%d%d" % (h, b)] = lambda: copy(out, bank)

        def parts(i, q, b):
            s["fs"[i] + q + str(b)] = lambda: pick(q, A("at%d" % i, b, 4 * K, 4), A("ta", AW * b, AW * b + C + 1), (ll, sn)[i])

        for b in range(4):
            element(b)
            for h in range(2):
                run(h)
                arrived(h, b)
                half(h)
                made(h, b)
                parts(h, "v", b)
                parts(h, "s", b)
        return s

    runs = [(CUT[h], CUT[h + 1]) for h in range(2)]
    for t in range(R):
        step = steps(t)
        for name in (START.split() if t == 0 else []) + ROUND.split():
            if t == 0 or name[0] != "*":
                step[name.strip("*")]()
        two(lb("WD", C, 2 * C, 4), lf("PS", 0, K), A("ps0", 1, P2, 2), ALU.is_lt)
        two(lb("WD", C + 3, 2 * C, 4), lf("PS", 0, K), A("ps0", 1, P2, 2), ALU.is_ge)
        for a, z in runs:
            two_at(lh("V", a, z), lb("WD", 0, 2 * C), lu("IDX", a // 16, z // 16), lf("HB", a, z), ALU.add)
        for a, z in runs:
            diagonal(lh("VR", a, z), lh("V", a, z), z - a, "D4")
        for a, z in runs:
            scalar1(lu("H4", a // 4, z // 4), lh("VR", a + 3, z, 4), 4.0, ALU.mult, lf("C4", 0, 1), ALU.add)
        for h in range(2):
            for q, a, z in DEAL[h]:
                pick(q, A("x%d" % (t + 1), 4 * a, 4 * z), A("tp", 0, 4 * TW), lu("H4", a // 4, z // 4))
            state(t + 1, h)
            scores(t + 1, h)
            if t + 1 == R:
                a, z = runs[h]
                dma("y", T.oc[:, 4 * a:4 * z], U8(A("qc3", a, z)), [], [A("qc3", a, z)])

    def scales(q, k):
        dma(q, T.osc[4 * k:4 * k + 4, :], T.qs3[32 * k:32 * k + 4, 0:C], [], [A("qs3", 0, C)])

    act(A("yt", 0, CUT[1]), A("ps4", 0, CUT[1]))
    dma("s", T.y[:, 0:CUT[1]], A("yt", 0, CUT[1])[0], [], [A("yt", 0, CUT[1])])
    copy(A("ott", 0, C), lh("V", 0, C))
    for k in range(3):
        scales("y", k)
    copy(A("yt", CUT[1], C), A("ps5", 0, C - CUT[1]))
    dma("s", T.y[:, CUT[1]:C], A("yt", CUT[1], C)[0], [], [A("yt", CUT[1], C)])
    scales("s", 3)
    dma("y", T.ot[:, :], T.ott[0:128:16, 0:C], [], [A("ott", 0, C)])
    close()
